import numpy as np, ml_dtypes
CORES = [9,25,41,57]
N = 4
import mx_ref
BF = ml_dtypes.bfloat16
def gentries(a):
    return np.ascontiguousarray(a.reshape(8, 16, -1).transpose(0, 2, 1)).reshape(8, -1)
def gtable(e):
    e = np.asarray(e); return np.ascontiguousarray(e.reshape(8, -1, 16).transpose(0, 2, 1)).reshape(128, -1).astype(np.int32)
def gcols(t, e):
    v = np.concatenate([t.reshape(8, 16, -1, 4), np.zeros((8, 16, 1, 4), BF)], axis=2)
    return np.ascontiguousarray(np.stack([v[g][:, e[g]] for g in range(8)])).reshape(128, -1)
def gpick(z, e):
    return np.concatenate([z[16 * g:16 * g + 16][:, e[g]] for g in range(8)])
def tile(rs):
    return np.stack(rs, axis=2).reshape(128, -1).astype(BF)
def pick(q, e):
    c = np.concatenate([q[0].reshape(128, -1, 4), np.zeros((128, 1, 4), np.uint8)], axis=1); s = np.concatenate([q[1], np.ones((16, 1), np.uint8)], axis=1)
    return (np.ascontiguousarray(c[:, e].reshape(128, -1)), np.ascontiguousarray(s[:, e]))
def join(*qs):
    return (np.concatenate([q[0] for q in qs], axis=1), np.concatenate([q[1] for q in qs], axis=1))
def put(q, e, v):
    c, s = q[0].reshape(128, -1, 4).copy(), q[1].copy(); c[:, e] = v[0].reshape(128, -1, 4); s[:, e] = v[1]
    return (c.reshape(128, -1), s)
def pk(c, s):
    return (np.ascontiguousarray(c), mx_ref.live(s))
def emit(q):
    return q[0], q[1]
def packed(v, rng):
    q = [mx_ref.quantize(np.ascontiguousarray(v[r])) for r in range(N)]
    return np.stack([a for a, b in q]), np.stack([mx_ref.plane(b, rng) for a, b in q])
def values_of_codes():
    e, c = np.zeros((128, 128, 4), np.float32), np.zeros((128, 2, 4), np.uint8)
    e[np.arange(128), np.arange(128), 0] = 1
    c[:127, :, 0] = np.arange(256).reshape(2, 128).T[:127]
    return mx_ref.matmul(mx_ref.quantize(e.reshape(128, 512).astype(BF)), (c.reshape(128, 8), np.full((16, 2), 127, np.uint8))).T.reshape(-1).astype(np.float64)
CODE_VALUE, SCALE_VALUE = values_of_codes(), 2.0 ** (np.arange(256) - 127.0)
def decode(q):
    return (CODE_VALUE[q[0]].reshape(16, 8, -1, 4) * SCALE_VALUE[q[1]][:, None, :, None] + 0.0).reshape(128, -1).astype(np.float32)
def f(rng, *shape):
    return mx_ref.flush((rng.standard_normal(shape, dtype=np.float32) * np.exp2(rng.integers(-2, 3, shape[:-1] + (1,)))).astype(BF))
def wide(rng, *shape, cols=0):
    v = rng.standard_normal(shape, dtype=np.float32) * np.exp2(rng.integers(-12, 13, shape)).astype(np.float32)
    if cols: v *= np.repeat(np.exp2(rng.integers(-cols, cols + 1, shape[:-2] + (1, shape[-1] // 4))) * (rng.random(shape[:-2] + (1, shape[-1] // 4)) > 0.0625), 4, axis=-1).astype(np.float32)
    return mx_ref.flush(v.astype(BF))
C, R = 448, 3
DECIDE = [0, 1, 2, 16, 32, 48, 64, 80, 96, 112]
def big(a):
    a = a.astype(np.float32)
    a[np.abs(a) < np.float32(2.0 ** -16)] = 0
    return a
def numbers_of(rng):
    return big(f(rng, N, 128, 4 * C)).reshape(N, 8, 16, C, 4), f(rng, N, 128, 512).astype(np.float32).reshape(N, 8, 16, 128, 4), f(rng, N, 128, 512).astype(np.float32).reshape(N, 8, 16, 128, 4)
def layers(rng, still=[]):
    w = np.clip(big(f(rng, N, 128, 2048)), -1, 1).reshape(N, 8, 16, 4, 8, 16, 4)
    w[:, :, still] = 0
    w[:, :, :, :, :, still] = 0
    return w
def inputs(rng, x, u, v, p, w):
    x, u, v, w = [np.ascontiguousarray(a).astype(np.float32).reshape(N, 128, -1).astype(BF) for a in (x, u, v, w)]
    c, s = packed(w, rng)
    return {"x": x, "u": u, "v": v, "p": np.stack([gtable(p[r]) for r in range(N)]), "wc": c, "ws": s}
def pointers(rng):
    return rng.integers(0, C, (N, 8, C))
def setup_inputs(rng):
    x, u, v = numbers_of(rng)
    return inputs(rng, x, u, v, pointers(rng), layers(rng))
def setup_inputs_ties(rng):
    x, u, v = numbers_of(rng)
    o = rng.permutation(N)
    k = rng.integers(0, 3, (N, 8, C, 4))
    k[:, :, :, 2] -= 1
    k[:, :, :, 3] = 0
    k[o[1], :, :, 2] = 1
    x[:, :, 0] = k
    h = np.ones(N)
    h[o[0]] = 0
    h[o[1]] = -1
    u[:, :, :, DECIDE] = 0
    for g in range(8): u[:, g, 0, 16 * g, 0] = h
    u[:, 0, 0, 1, 1] = 1
    u[:, 0, 0, 2, 2] = 1
    u[o[2], :, :, 1] = 0
    u[o[3], :, :, 2] = 0
    return inputs(rng, x, u, v, pointers(rng), layers(rng, [0]))
def setup_inputs_near(rng):
    x, u, v = numbers_of(rng)
    hold = [0, 1] + [i for i in range(8, 16)]
    x[:, :, hold] = 0
    u[:, :, :, DECIDE] = 0
    o = rng.permutation(N) % 4
    e = 2.0 ** -30
    for r in range(N):
        k = 1.0 if o[r] == 0 else e
        s, n = rng.integers(0, 16, (8, C)), rng.integers(0, 16, C)
        c, m = rng.integers(0, 2, C) * 2.0 - 1.0, rng.integers(0, 2, C) * 2.0 - 1.0
        z = rng.integers(-1, 2, C)
        x[r, :, 8] = ((s[:, :, None] >> np.arange(4)) & 1) * np.exp2(np.arange(4) - 23.0)
        x[r, 0, 9] = ((n[:, None] >> np.arange(4)) & 1) * np.exp2(np.arange(4) - 23.0)
        if o[r] < 2:
            x[r, :, 0, :, 0] = c
            x[r, :, 11, :, 0] = 2.0 ** -10
            x[r, 0, 1, :, 0] = m
            x[r, 0, 12, :, 0] = 2.0 ** -10
            x[r, 1, 9, :, 0] = z * 2.0 ** -23
            u[r, 0, 1, 1, 0] = k
            u[r, 0, 12, 1, 0] = k
            u[r, 1, 9, 2, 0] = k
        elif o[r] == 2:
            x[r, :, 0, :, 0] = np.where(c < 0, -1.0, 0.0)
            x[r, 0, 1, :, 0] = np.where(rng.permutation(C) % 8 == 0, m, 0.0)
            x[r, 1, 13, :, 0] = z * e
            u[r, 0, 1, 1, 0] = 1
            u[r, 1, 13, 2, 0] = e
        else:
            x[r, :, 10, :, 0] = rng.integers(1, 3, (8, C)) * c * np.where(np.arange(8) < 4, e, 1.125 * e)[:, None]
            x[r, 0, 14, :, 0] = rng.integers(-2, 3, C) * e
            x[r, 1, 13, :, 0] = z * 1.125 * e
            x[r, 1, 14, :, 0] = (0 - z) * 1.25 * e
            u[r, 0, 14, 1, 0] = e
            u[r, 1, 13, 2, 0] = 1.125 * e
            u[r, 1, 14, 2, 0] = e
        if o[r] < 3: u[r, 0, 9, 1] = k
        far = rng.permutation(8)
        for g in range(8):
            if o[r] < 2:
                u[r, g, 0, 16 * g, 0] = k
                u[r, g, 11, 16 * g, 0] = k
            if o[r] == 2 and g in far[:2]: u[r, g, 0, 16 * g, 0] = 1
            if o[r] < 3: u[r, g, 8, 16 * g] = k
            else: u[r, g, 10, 16 * g, 0] = 1.25 * e if g < 4 else 1.125 * e
    return inputs(rng, x, u, v, pointers(rng), layers(rng, hold))
def setup_inputs_late(rng):
    x, u, v = numbers_of(rng)
    x[:, :, 0] = (rng.permutation(N) % 2 * 0.0625)[:, None, None, None]
    u[:, :, :, DECIDE] = 0
    for g in range(8): u[:, g, 0, 16 * g, 0] = 1
    u[:, 0, 0, 1, 1] = 1
    u[:, 0, 0, 2, 2] = 1
    return inputs(rng, x, u, v, pointers(rng), layers(rng))
def setup_inputs_ends(rng):
    x, u, v = numbers_of(rng)
    o, h = rng.permutation(N), rng.permutation(8)
    p = pointers(rng)
    x[:] = np.where(rng.random((N, 8, 1, C, 1)) < 0.5, 0.875, 1.0) * 2.0 ** 25
    v[:] = (rng.integers(0, 2, (N, 1, 1, 128, 1)) * 2.0 - 1.0) * 2.0 ** 30
    u[:, :, :, DECIDE] = 2.0 ** 30
    for g in range(8): u[:, g, :, 16 * g] = 2.0 ** 29
    u[:, :, :, 2] = 0
    u[:, 0, :, 2] = 2.0 ** 30
    u[:, 1, :, 2] = -2.0 ** 30
    p[o[0]] = C - 1
    x[o[0], :, :, :C - 1] = 2.0 ** -30
    u[o[0], :, :, 2] = -2.0 ** 30
    p[o[1]] = 0
    x[o[1]] = 2.0 ** 25
    u[o[1], :, :, ::16] = 2.0 ** 30
    u[o[1], :, :, 2] = 2.0 ** 30
    p[o[2], h[:4]] = C - 1
    p[o[2], h[4:]] = 0
    p[o[2], 0] = rng.permutation(C)
    x[o[2], :, :, 1 + rng.permutation(C - 2)[:C // 2]] = 2.0 ** -30
    u[o[2], :, :, ::16] = -2.0 ** 30
    u[o[2], 0, :, 112] = -2.0 ** 29
    u[o[2], :, :, 1] *= -1
    u[o[2], :, :, 2] = 2.0 ** 30
    for g in h[:4]: u[o[3], :, :, 16 * g] *= -1
    u[o[3], :, :, 3:16] = 2.0 ** -30
    v[o[3]] = 2.0 ** -30
    return inputs(rng, x, u, v, p, np.ones((N, 128, 2048)))
def setup_inputs_spread(rng):
    x, u, v = numbers_of(rng)
    return inputs(rng, big(wide(rng, N, 128, 4 * C, cols=6)), u, v, pointers(rng), layers(rng))
def check_inputs(d):
    b = []
    for k, top in (("x", 2.0 ** 25), ("u", 2.0 ** 30), ("v", 2.0 ** 30)):
        a = np.abs(d[k].astype(np.float32))
        if not (np.isfinite(a).all() and ((a == 0) | (a >= 2.0 ** -30) & (a <= top)).all()): b.append("a value of " + k)
    if not ((d["p"] >= 0) & (d["p"] < C)).all(): b.append("an entry of p")
    none, least, most = [emit(mx_ref.quantize(np.full((128, 16), k, np.float32).astype(BF)))[1][0, 0] for k in (0.0, 2.0 ** -30, 1.0)]
    for r in range(N):
        if ((d["wc"][r] == 0x7F) | (d["wc"][r] == 0xFF)).any(): b.append("wc: a code that is no number")
        s = mx_ref.live(d["ws"][r])
        if ((s != none) & ((s < least) | (s > most))).any(): b.append("ws: a scale out of range")
        with np.errstate(all="ignore"):
            if not (np.abs(decode(pk(d["wc"][r], d["ws"][r]))) <= 1).all(): b.append("a number of W beyond 1 in size")
    return b
def reference(x, u, v, p, wc, ws):
    qu = [mx_ref.quantize(u[r]) for r in range(N)]
    lay = [pk(wc[r], ws[r]) for r in range(N)]
    first = np.stack([gentries(p[r]) for r in range(N)])
    ptr = first.copy()
    now = [x[r] for r in range(N)]
    g, j = np.arange(8)[:, None], np.arange(C)
    for t in range(R):
        sent, via = [], []
        for r in range(N):
            s = mx_ref.matmul(qu[r], mx_ref.quantize(now[r])) + np.float32(0.0)
            level = np.argmax(s[::16], axis=0)
            o = np.argsort(-s[1], kind="stable")
            c = np.zeros(C, np.int64)
            c[o] = np.roll(o, -1)
            call = s[2] > 0
            new = np.where((g < level) & call, ptr[r][:, c], ptr[r])
            new = np.where(g == level, np.where(call, j, first[r]), new)
            ptr[r] = new
            via.append(new[:, c])
            sent.append(mx_ref.quantize(gcols(now[r], new)))
        for r in range(N):
            q = sent[(r - 1 - t) % N]
            h = [mx_ref.matmul(pick(lay[r], np.arange(128 * b, 128 * b + 128)), q) * np.float32(0.00390625) for b in range(4)]
            now[r] = tile([gpick(h[b], via[r]) + now[r][:, b::4].astype(np.float32) for b in range(4)])
    y, op = np.zeros((N, 128, C), np.float32), np.zeros((N, 8, C), np.float32)
    oc, osc = np.zeros((N, 128, 4 * C), np.uint8), np.zeros((N, 16, C), np.uint8)
    for r in range(N):
        q = mx_ref.quantize(now[r])
        y[r] = mx_ref.matmul(mx_ref.quantize(v[r]), q)
        op[r] = ptr[r]
        oc[r], osc[r] = emit(q)
    return {"y": y, "op": op, "oc": oc, "osc": osc}

@@ -1,0 +1,412 @@
+from concourse.mybir import dt, AluOpType as A, ActivationFunctionType as F
+
+C, R, N = 448, 3, 4
+H = [(0, 256), (256, 448)]
+BIG = -1.0e29
+
+SCRATCH = {
+    "PS": ("psum", [128, 4096], "float32"),
+    "UT": ("sbuf", [128, 512], "bfloat16"), "VT": ("sbuf", [128, 512], "bfloat16"), "ZT": ("sbuf", [128, 512], "bfloat16"),
+    "QU": ("sbuf", [128, 128], "float8_e4m3fn_x4"), "QUS": ("sbuf", [128, 128], "uint8"),
+    "QU1": ("sbuf", [128, 128], "float8_e4m3fn_x4"), "QU1S": ("sbuf", [128, 128], "uint8"),
+    "QV": ("sbuf", [128, 128], "float8_e4m3fn_x4"), "QVS": ("sbuf", [128, 128], "uint8"),
+    "WC": ("sbuf", [128, 512], "float8_e4m3fn_x4"), "WS": ("sbuf", [128, 512], "uint8"),
+    "QX": ("sbuf", [128, 512], "float8_e4m3fn_x4"), "QXS": ("sbuf", [128, 512], "uint8"),
+    "PI": ("sbuf", [128, 28], "int32"), "PIX": ("sbuf", [128, 1], "int32"), "PMI": ("sbuf", [128, 1], "int32"), "GI": ("sbuf", [128, 1], "int32"),
+    "PM": ("sbuf", [128, 1], "float32"), "PF": ("sbuf", [128, 1], "float32"), "NG": ("sbuf", [128, 1], "float32"), "NG16": ("sbuf", [128, 1], "float32"),
+    "IO": ("sbuf", [128, 448], "float32"), "MD": ("sbuf", [128, 448], "float32"), "MASK": ("sbuf", [128, 448], "float32"),
+    "A16": ("sbuf", [128, 28], "float32"), "DB": ("sbuf", [128, 4], "float32"), "DUPL": ("sbuf", [128, 4], "uint16"),
+    "U1L": ("sbuf", [128, 8], "uint16"), "THR": ("sbuf", [128, 128], "bfloat16"),
+    "Z8": ("sbuf", [128, 8], "float32"), "JW": ("sbuf", [128, 28], "float32"), "PW": ("sbuf", [128, 28], "float32"), "JP": ("sbuf", [128, 28], "float32"),
+    "D16": ("sbuf", [128, 28], "uint16"), "NS": ("sbuf", [128, 4], "float32"),
+    "RUN": ("sbuf", [128, 32], "float32"), "LJ": ("sbuf", [128, 32], "float32"), "LV": ("sbuf", [128, 4], "float32"), "CF": ("sbuf", [128, 4], "float32"),
+    "SG": ("sbuf", [128, 1792], "bfloat16"), "CM": ("sbuf", [128, 1792], "bfloat16"), "SCN": ("sbuf", [128, 1792], "bfloat16"),
+    "NAT": ("sbuf", [128, 32], "float32"), "TT": ("sbuf", [128, 32], "float32"), "LT": ("sbuf", [128, 64], "float32"), "L2": ("sbuf", [128, 64], "float32"),
+    "LR": ("sbuf", [128, 64], "float32"), "RK": ("sbuf", [128, 28], "uint16"), "RK1": ("sbuf", [128, 28], "uint16"),
+    "PD": ("sbuf", [128, 456], "float32"), "RM": ("sbuf", [128, 448], "float32"), "SC": ("sbuf", [128, 232], "float32"),
+    "a1": ("sbuf", [128, 28], "float32"), "al": ("sbuf", [128, 28], "float32"), "b1": ("sbuf", [128, 28], "float32"),
+    "a2": ("sbuf", [128, 28], "float32"), "b2": ("sbuf", [128, 28], "float32"),
+    "m1": ("sbuf", [128, 28], "float32"), "m2": ("sbuf", [128, 28], "float32"), "m3": ("sbuf", [128, 28], "float32"),
+    "k1": ("sbuf", [128, 28], "float32"), "k2": ("sbuf", [128, 28], "float32"), "k3": ("sbuf", [128, 28], "float32"),
+    "dc": ("sbuf", [128, 28], "float32"), "u1": ("sbuf", [128, 28], "float32"), "ED": ("sbuf", [128, 28], "float32"), "EL": ("sbuf", [128, 28], "uint16"),
+    "JD": ("sbuf", [128, 28], "float32"), "PDF": ("sbuf", [128, 28], "float32"), "KK": ("sbuf", [128, 28], "float32"),
+    "Z": ("sbuf", [128, 1792], "bfloat16"), "YS": ("sbuf", [128, 448], "float32"),
+}
+for _i in range(4):
+    SCRATCH["X%d" % _i] = ("sbuf", [128, 1792], "bfloat16")
+    SCRATCH["DR%d" % _i] = ("sbuf", [128, 448], "float32")
+    SCRATCH["D%d" % _i] = ("sbuf", [128, 28], "float32")
+    SCRATCH["OF%d" % _i] = ("sbuf", [128, 28], "uint16")
+    SCRATCH["HS%d" % _i] = ("sbuf", [128, 448], "float32")
+for _i in range(R):
+    SCRATCH["QZ%d" % _i] = ("sbuf", [128, 448], "float8_e4m3fn_x4")
+    SCRATCH["QZS%d" % _i] = ("sbuf", [128, 448], "uint8")
+    SCRATCH["LZ%d" % _i] = ("sbuf", [128, 448], "float8_e4m3fn_x4")
+    SCRATCH["LS%d" % _i] = ("sbuf", [128, 448], "uint8")
+
+SEMAPHORES = ["sv", "ss", "st", "sg", "loc"]
+SEMAPHORES += ["ld%d" % _i for _i in range(8)] + ["sto%d" % _i for _i in range(12)]
+SEMAPHORES += ["ar%d%d%s" % (_t, _h, _k) for _t in range(R) for _h in range(2) for _k in "cs"]
+
+
+def rank_program(g, core, T, topo):
+    rank = T.rank_of(core)
+    if rank is None:
+        return
+    q = {"v": g.vector, "s": g.scalar, "t": g.tensor, "g": g, "y": g.sync}
+    own = {"v": "sv", "s": "ss", "t": "st", "g": "sg"}
+    cnt, known, clock, lastw, readers = {}, {k: {} for k in q}, {}, {}, {}
+
+    def waits(qn, reads, writes):
+        need = {}
+        for k in reads:
+            if k in lastw:
+                s, n, _ = lastw[k]
+                need[s] = max(need.get(s, 0), n)
+        for k in writes:
+            if k in lastw:
+                s, n, _ = lastw[k]
+                need[s] = max(need.get(s, 0), n)
+            for s, n, rq in readers.get(k, []):
+                if rq != qn:
+                    need[s] = max(need.get(s, 0), n)
+        kn = known[qn]
+        need = {s: n for s, n in need.items() if kn.get(s, 0) < n}
+        for s in list(need):
+            if any(o != s and clock.get((o, need[o]), {}).get(s, 0) >= need[s] for o in need):
+                del need[s]
+        for s, n in need.items():
+            q[qn].wait_ge(T.sem[s], n)
+            for o, m in clock.get((s, n), {}).items():
+                kn[o] = max(kn.get(o, 0), m)
+            kn[s] = max(kn.get(s, 0), n)
+
+    def note(qn, reads, writes, s, n, dma):
+        clock[(s, n)] = dict(known[qn])
+        for k in writes:
+            lastw[k] = (s, n, qn)
+            readers[k] = []
+        for k in reads:
+            readers.setdefault(k, []).append((s, n, None if dma else qn))
+
+    def do(qn, fn, args, reads, writes, **kw):
+        waits(qn, reads, writes)
+        s = own[qn]
+        n = cnt.get(s, 0) + 1
+        cnt[s] = n
+        fn(*args, **kw).then_inc(T.sem[s], 1)
+        note(qn, reads, writes, s, n, False)
+
+    def dma(qn, s, out, in_, reads, writes):
+        waits(qn, reads, writes)
+        q[qn].dma_start(out, in_).then_inc(T.sem[s], 16)
+        cnt[s] = 16
+        note(qn, reads, writes, s, 16, True)
+
+    V, S, TE = g.vector, g.scalar, g.tensor
+
+    def ts(out, in0, s1, s2, ops, reads, writes):
+        do("v", V.tensor_scalar, (out, in0, s1, s2) + tuple(ops), reads, writes)
+
+    def tt(out, a, b, op, reads, writes):
+        do("v", V.tensor_tensor, (out, a, b, op), reads, writes)
+
+    def vcopy(out, a, reads, writes):
+        do("v", V.tensor_copy, (out, a), reads, writes)
+
+    def act(out, a, f, reads, writes, **kw):
+        do("s", S.activation, (out, a, f), reads, writes, **kw)
+
+    def scan(out, a, b, init, o0, o1, reads, writes):
+        do("v", V.tensor_tensor_scan, (out, a, b, init, o0, o1), reads, writes)
+
+    def quant(oc, os_, tile, reads, writes):
+        do("v", V.quantize_mx, (oc, os_, tile), reads, writes)
+
+    def mm(bank, n, l, ls, r, rs, reads):
+        do("t", TE.matmul_mx, (T.PS[:, 512 * bank:512 * bank + n], l, ls, r, rs, True, True), reads, ["bk%d" % bank])
+
+    def fill(ap, c, key):
+        do("v", V.memset, (ap, c), [], [key])
+
+    dma("y", "ld0", T.X0[:, 0:1024], T.x[:, 0:1024], [], ["X0h0"])
+    dma("s", "ld1", T.UT[:, :], T.u[:, :], [], ["UT"])
+    dma("s", "ld2", T.PI[:, :], T.p[:, :], [], ["PI"])
+    dma("y", "ld3", T.X0[:, 1024:1792], T.x[:, 1024:1792], [], ["X0h1"])
+    dma("y", "ld4", T.WC[:, :].bitcast(dt.uint8), T.wc[:, :], [], ["WC"])
+    dma("y", "ld5", T.WS[:, :], T.ws[:, :], [], ["WS"])
+    dma("y", "ld6", T.VT[:, :], T.v[:, :], [], ["VT"])
+
+    do("g", g.iota, (T.PIX[:, :], [[0, 1]], 0, 1), [], ["PIX"])
+    do("g", g.iota, (T.DB[:, :], [[16, 2], [0, 2]], 0, 0), [], ["DB"], allow_small_or_imprecise_dtypes=True)
+    do("g", g.iota, (T.A16[:, :], [[16, 28]], 0, 0), [], ["A16"], allow_small_or_imprecise_dtypes=True)
+    do("g", g.iota, (T.IO[:, :], [[1, 448]], 0, 0), [], ["IO"], allow_small_or_imprecise_dtypes=True)
+    do("g", g.iota, (T.MD[:, :], [[0, 28], [1, 16]], 0, 0), [], ["MD"], allow_small_or_imprecise_dtypes=True)
+    fill(T.U1L[:, :], 1, "U1L")
+    fill(T.ZT[:, :], 0.0, "ZT")
+    fill(T.Z8[:, :], 0.0, "Z8")
+    fill(T.SC[:, :], 0.0, "SC")
+    fill(T.PD[:, :], 0.0, "PD")
+    fill(T.TT[:, :], 0.0, "TT")
+    quant(T.QX[:, 384:512], T.QXS[:, 384:512], T.ZT[:, :], ["ZT"], ["QXh1", "QXz"])
+    ts(T.PMI[:, :], T.PIX[:, :], 15, None, [A.bitwise_and], ["PIX"], ["PMI"])
+    ts(T.GI[:, :], T.PIX[:, :], 4, None, [A.arith_shift_right], ["PIX"], ["GI"])
+    vcopy(T.PF[:, :], T.PIX[:, :], ["PIX"], ["PF"])
+    vcopy(T.PM[:, :], T.PMI[:, :], ["PMI"], ["PM"])
+    ts(T.NG[:, :], T.GI[:, :], -1.0, None, [A.mult], ["GI"], ["NG"])
+    ts(T.NG16[:, :], T.GI[:, :], -1.0, -16.0, [A.mult, A.add], ["GI"], ["NG16"])
+    ts(T.DUPL[:, :], T.DB[:, :], T.PM[:, 0:1], None, [A.add], ["DB", "PM"], ["DUPL"])
+    ts(T.JW[:, :], T.A16[:, :], T.PM[:, 0:1], None, [A.add], ["A16", "PM"], ["JW"])
+
+    quant(T.QU[:, :], T.QUS[:, :], T.UT[:, :], ["UT"], ["QU"])
+    vcopy(T.QU1[:, :].bitcast(dt.uint32), T.QU[:, 0:128].bitcast(dt.uint32).indirect(T.U1L[:, 0:8]), ["QU", "U1L"], ["QU1c"])
+    vcopy(T.QU1S[:, :], T.QUS[:, 0:128].indirect(T.U1L[:, 0:8]), ["QU", "U1L"], ["QU1s"])
+
+    def quant_x(t, h):
+        a, b = H[h]
+        quant(T.QX[:, a:b], T.QXS[:, a:b], T["X%d" % t][:, 4 * a:4 * b], ["X%dh%d" % (t, h)], ["QXh%d" % h])
+
+    def products(h):
+        a, b = H[h]
+        for m in (0, 1) if h == 0 else (2, 3):
+            mm(m, 128, T.QX[:, 128 * m:128 * m + 128], T.QXS[:, 128 * m:128 * m + 128], T.QU[:, :], T.QUS[:, :],
+               ["QXh%d" % h, "QU"] + (["QXz"] if m == 3 else []))
+        mm(4 + h, b - a, T.QU1[:, :], T.QU1S[:, :], T.QX[:, a:b], T.QXS[:, a:b], ["QXh%d" % h, "QU1c", "QU1s"])
+
+    def negs(m):
+        ts(T.NS[:, m:m + 1], T.PS[:, 512 * m + 1:512 * m + 2], -1.0, None, [A.mult], ["bk%d" % m], ["NS%d" % m])
+
+    def sign(m, h):
+        a, b = H[h]
+        act(T.SG[:, 448 * m + a:448 * m + b], T.PS[:, 512 * (4 + h):512 * (4 + h) + b - a], F.Sign,
+            ["bk%d" % (4 + h), "NS%d" % m], ["SG%d%d" % (m, h)], bias=T.NS[:, m:m + 1])
+
+    def runmax(m):
+        scan(T.RUN[:, 8 * m:8 * m + 8], T.Z8[:, :], T.PS[:, 512 * m:512 * m + 128:16], BIG, A.add, A.max, ["Z8", "bk%d" % m], ["RUN%d" % m])
+
+    def level(m):
+        act(T.LJ[:, 8 * m:8 * m + 8], T.RUN[:, 8 * m:8 * m + 8], F.Sign, ["RUN%d" % m], ["LJ%d" % m, "LV%d" % m],
+            bias=T.RUN[:, 8 * m + 7:8 * m + 8], scale=-1.0, accum_out=T.LV[:, m:m + 1])
+
+    def before(m, a, b, kind):
+        o = 448 * m
+        hs = [h for h in (0, 1) if a < H[h][1] and b > H[h][0]]
+        rd = ["SG%d%d" % (m, h) for h in hs]
+        if kind == "tri":
+            tt(T.CM[:, o + a:o + b], T.SG[:, o + a:o + b], T.THR[:, 0:b - a], A.is_gt, rd + ["THR"], ["CM%d.%d" % (m, a)])
+        else:
+            ts(T.CM[:, o + a:o + b], T.SG[:, o + a:o + b], 0.0, None, [kind], rd, ["CM%d.%d" % (m, a)])
+
+    def count(m, parts):
+        o = 448 * m
+        scan(T.SCN[:, 224 * m:224 * m + 224], T.CM[:, o:o + 224], T.CM[:, o + 224:o + 448], -225.0, A.add, A.add,
+             ["CM%d.%d" % (m, a) for a in parts], ["SCN%d" % m])
+
+    def successor(src, dst):
+        vcopy(T.PD[:, 0:448].indirect(T.RK[:, 0:28]), src[0], ["RK", src[1]], ["PD"])
+        return dst
+
+    def succ_gather():
+        vcopy(T.PD[:, 448:449], T.PD[:, 0:1], ["PD"], ["PD"])
+        tt(T.RM[:, :], T.PD[:, 0:456].indirect(T.RK1[:, 0:28]), T.MASK[:, :], A.mult, ["PD", "RK1", "MASK"], ["RM"])
+
+    def succ_sum():
+        scan(T.SC[:, 1:225], T.RM[:, 0:448:2], T.RM[:, 1:448:2], 0.0, A.add, A.add, ["RM"], ["SC"])
+
+    def succ_diff(dst, key):
+        tt(dst, T.SC[:, 8:225:8], T.SC[:, 0:217:8], A.subtract, ["SC"], [key])
+
+    def scores_tail():
+        runmax(0); runmax(1)
+        negs(2); negs(3)
+        for m in (2, 3):
+            sign(m, 0)
+        level(0); level(1)
+        before(0, 0, 128, "tri")
+        before(1, 0, 128, A.is_ge)
+        before(1, 128, 256, "tri")
+        runmax(2); runmax(3)
+        ts(T.CF[:, :], T.PS[:, 2:2048:512], 0.0, 16.0, [A.is_gt, A.mult], ["bk0", "bk1", "bk2", "bk3"], ["CF"])
+        for m in range(4):
+            sign(m, 1)
+            if m == 1:
+                level(2); level(3)
+        before(2, 0, 256, A.is_ge)
+        before(3, 0, 256, A.is_ge)
+        before(0, 128, 448, A.is_gt)
+        count(0, [0, 128])
+        before(1, 256, 448, A.is_gt)
+        count(1, [0, 128, 256])
+        tt(T.SCN[:, 1119:1792:224], T.LV[:, :], T.CF[:, :], A.add, ["LV0", "LV1", "LV2", "LV3", "CF"], ["SCNw"])
+        before(2, 256, 384, "tri")
+        before(2, 384, 448, A.is_gt)
+        count(2, [0, 256, 384])
+        before(3, 256, 384, A.is_ge)
+        before(3, 384, 448, "tri")
+        count(3, [0, 256, 384])
+
+    def wrapped():
+        rd = ["SCN0", "SCN1", "SCN2", "SCN3", "SCNw"]
+        for b in range(4):
+            o, i = T.NAT[0:32, b:32:4], T.SCN[32 * b:32 * b + 32, 223:1792:224]
+            if b < 2:
+                vcopy(o, i, rd, ["NAT%d" % b])
+            else:
+                act(o, i, F.Copy, rd, ["NAT%d" % b])
+        do("v", V.transpose, (T.TT[0:32, 0:32], T.NAT[0:32, 0:32]), ["NAT0", "NAT1", "NAT2", "NAT3"], ["TT"])
+        vcopy(T.LT[:, :], T.TT[:, 0:32].indirect(T.DUPL[:, 0:4]), ["TT", "DUPL"], ["LT"])
+        do("v", V.transpose, (T.L2[0:32, 0:64], T.LT[0:32, 0:64]), ["LT"], ["L2"])
+        for b in range(4):
+            vcopy(T.LR[32 * b:32 * b + 32, 0:64:2], T.L2[0:32, 0:32], ["L2"], ["LR0%d" % b])
+            act(T.LR[32 * b:32 * b + 32, 1:64:2], T.L2[0:32, 32:64], F.Copy, ["L2"], ["LR1%d" % b])
+
+    LRK = ["LR%d%d" % (e, b) for e in range(2) for b in range(4)]
+
+    def prep(t):
+        d = T["D%d" % t][:, :] if t else T.PW[:, :]
+        k = "D%d" % t if t else "PW"
+        tt(T.JD[:, :], T.JW[:, :], d, A.subtract, ["JW", k], ["JD"])
+        tt(T.PDF[:, :], T.PW[:, :], d, A.subtract, ["PW", k], ["PDF"])
+        tt(T.KK[:, :], T.JP[:, :], d, A.subtract, ["JP", k], ["KK"])
+
+    def pointers(t):
+        d = T["D%d" % t][:, :] if t else T.PW[:, :]
+        k = "D%d" % t if t else "PW"
+        W = T.LR[:, 32:60]
+        ts(T.RK[:, :], T.LR[:, 0:28], 224.0, None, [A.add], LRK, ["RK"])
+        vcopy(T.PD[:, 0:448].indirect(T.RK[:, 0:28]), T["DR%d" % t][:, :], ["RK", "DR%d" % t], ["PD"])
+        act(T.a1[:, :], W, F.Sign, LRK + ["NG16"], ["a1"], bias=T.NG16[:, 0:1])
+        act(T.a2[:, :], W, F.Sign, LRK + ["NG"], ["a2"], bias=T.NG[:, 0:1])
+        act(T.b1[:, :], T.a1[:, :], F.Square, ["a1"], ["b1"])
+        act(T.b2[:, :], T.a2[:, :], F.Square, ["a2"], ["b2"])
+        act(T.al[:, :], T.a1[:, :], F.Relu, ["a1"], ["al"])
+        ts(T.RK1[:, :], T.LR[:, 0:28], 225.0, None, [A.add], LRK, ["RK1"])
+        succ_gather()
+        tt(T.m1[:, :], T.b1[:, :], T.JD[:, :], A.mult, ["b1", "JD"], ["m1"])
+        tt(T.m2[:, :], T.b2[:, :], T.PDF[:, :], A.mult, ["b2", "PDF"], ["m2"])
+        tt(T.m3[:, :], T.al[:, :], d, A.mult, ["al", k], ["m3"])
+        succ_sum()
+        tt(T.k1[:, :], T.KK[:, :], T.m1[:, :], A.subtract, ["KK", "m1"], ["k1"])
+        tt(T.k2[:, :], T.m2[:, :], T.m3[:, :], A.add, ["m2", "m3"], ["k2"])
+        succ_diff(T.dc[:, :], "dc")
+        tt(T.k3[:, :], T.k1[:, :], T.k2[:, :], A.subtract, ["k1", "k2"], ["k3"])
+        tt(T.u1[:, :], T.al[:, :], T.dc[:, :], A.mult, ["al", "dc"], ["u1"])
+        n = "D%d" % (t + 1)
+        tt(T[n][:, :], T.u1[:, :], T.k3[:, :], A.add, ["u1", "k3"], [n])
+        for e in (2, 0, 3, 1):
+            ts(T["OF%d" % e][:, :], T[n][:, :], 4.0, float(e), [A.mult, A.add], [n], ["OF%d" % e])
+
+    def send(t, h):
+        a, b = H[h]
+        dst = T.cores[(rank + 1 + t) % N]
+        rid, pid, _ = topo.addr(dst)
+        m = topo.mask(core, dst)
+        waits("g", ["QZ%dh%d" % (t, h)], [])
+        g.remote_dma(T["LZ%d" % t][:, a:b].bitcast(dt.uint8), T["QZ%d" % t][:, a:b].bitcast(dt.uint8),
+                     T.sem["ar%d%dc" % (t, h)], T.sem.loc, pid, rid, m)
+        g.remote_dma(T["LS%d" % t][:, a:b], T["QZS%d" % t][:, a:b], T.sem["ar%d%ds" % (t, h)], T.sem.loc, pid, rid, m)
+        e = len(topo.engines(core, dst))
+        cnt["loc"] = cnt.get("loc", 0) + 2 * e
+        src = T.cores[(rank - 1 - t) % N]
+        e = len(topo.engines(src, core))
+        lastw["LZ%dh%d" % (t, h)] = ("ar%d%dc" % (t, h), e, None)
+        lastw["LS%dh%d" % (t, h)] = ("ar%d%ds" % (t, h), e, None)
+
+    def mosaic(t):
+        X = T["X%d" % t]
+        xk = ["X%dh0" % t, "X%dh1" % t]
+        n = "D%d" % (t + 1)
+        for h in range(2):
+            a, b = H[h]
+            for e in (2, 3):
+                act(T.Z[:, 4 * a + e:4 * b:4], X[:, 0:1792].indirect(T["OF%d" % e][:, a // 16:b // 16]), F.Copy,
+                    xk + ["OF%d" % e], ["Zh%d.%d" % (h, e)])
+            for e in (0, 1):
+                vcopy(T.Z[:, 4 * a + e:4 * b:4], X[:, 0:1792].indirect(T["OF%d" % e][:, a // 16:b // 16]),
+                      xk + ["OF%d" % e], ["Zh%d.%d" % (h, e)])
+            quant(T["QZ%d" % t][:, a:b], T["QZS%d" % t][:, a:b], T.Z[:, 4 * a:4 * b],
+                  ["Zh%d.%d" % (h, e) for e in range(4)], ["QZ%dh%d" % (t, h)])
+            send(t, h)
+            if h == 0:
+                vcopy(T.D16[:, :], T[n][:, :], [n], ["D16"])
+        act(T["DR%d" % (t + 1)][:, :], T.IO[:, 0:448].indirect(T.D16[:, 0:28]), F.Copy, ["IO", "D16"], ["DR%d" % (t + 1)])
+
+    def join_list(t):
+        if t < R - 1:
+            prep(t + 1)
+        vcopy(T.PD[:, 0:448].indirect(T.RK[:, 0:28]), T["DR%d" % (t + 1)][:, :], ["RK", "DR%d" % (t + 1)], ["PD"])
+        succ_gather()
+        succ_sum()
+        succ_diff(T.ED[:, :], "ED")
+        vcopy(T.EL[:, :], T.ED[:, :], ["ED"], ["EL"])
+
+    def layer(t):
+        for h in range(2):
+            a, b = H[h]
+            for w in range(4):
+                mm(2 * w + h, b - a, T.WC[:, 128 * w:128 * w + 128], T.WS[:, 128 * w:128 * w + 128], T["LZ%d" % t][:, a:b], T["LS%d" % t][:, a:b],
+                   ["WC", "WS", "LZ%dh%d" % (t, h), "LS%dh%d" % (t, h)])
+                bk = 2 * w + h
+                act(T["HS%d" % w][:, a:b], T.PS[:, 512 * bk:512 * bk + b - a], F.Copy, ["bk%d" % bk], ["HS%dh%d" % (w, h)], scale=0.00390625)
+
+    def join(t, h, w):
+        a, b = H[h]
+        tt(T["X%d" % (t + 1)][:, 4 * a + w:4 * b:4], T["HS%d" % w][:, 0:448].indirect(T.EL[:, a // 16:b // 16]),
+           T["X%d" % t][:, 4 * a + w:4 * b:4], A.add, ["HS%dh0" % w, "HS%dh1" % w, "EL", "X%dh%d" % (t, h)], ["X%dh%d.%d" % (t + 1, h, w)])
+        if w == 3:
+            lastw["X%dh%d" % (t + 1, h)] = lastw["X%dh%d.3" % (t + 1, h)]
+
+    quant_x(0, 0)
+    products(0)
+    ts(T.THR[:, :], T.IO[:, 0:128], T.PF[:, 0:1], 0.5, [A.is_gt, A.subtract], ["IO", "PF"], ["THR"])
+    negs(0); negs(1)
+    sign(0, 0); sign(1, 0)
+    quant_x(0, 1)
+    products(1)
+    vcopy(T.PW[:, :], T.PI[:, :], ["PI"], ["PW"])
+    vcopy(T.D16[:, :], T.PI[:, :], ["PI"], ["D16"])
+    scores_tail()
+    act(T.DR0[:, :], T.IO[:, 0:448].indirect(T.D16[:, 0:28]), F.Copy, ["IO", "D16"], ["DR0"])
+    tt(T.JP[:, :], T.JW[:, :], T.PW[:, :], A.add, ["JW", "PW"], ["JP"])
+    prep(0)
+    ts(T.MASK[:, :], T.MD[:, :], T.PM[:, 0:1], None, [A.is_equal], ["MD", "PM"], ["MASK"])
+
+    for t in range(R):
+        wrapped()
+        pointers(t)
+        mosaic(t)
+        join_list(t)
+        layer(t)
+        if t == 0:
+            quant(T.QV[:, :], T.QVS[:, :], T.VT[:, :], ["VT"], ["QV"])
+        for w in range(4):
+            join(t, 0, w)
+        quant_x(t + 1, 0)
+        if t < R - 1:
+            products(0)
+            join(t, 1, 0)
+            negs(0); negs(1)
+            sign(0, 0); sign(1, 0)
+            for w in (1, 2, 3):
+                join(t, 1, w)
+            quant_x(t + 1, 1)
+            products(1)
+            scores_tail()
+    dma("y", "sto0", T.op[:, :], T.DR3[0:128:16, :], ["DR3"], ["op"])
+    dma("y", "sto1", T.oc[:, 0:1024], T.QX[:, 0:256].bitcast(dt.uint8), ["QXh0"], ["oc0"])
+    mm(6, 256, T.QV[:, :], T.QVS[:, :], T.QX[:, 0:256], T.QXS[:, 0:256], ["QV", "QXh0"])
+    act(T.YS[:, 0:256], T.PS[:, 3072:3328], F.Copy, ["bk6"], ["YS0"])
+    dma("y", "sto2", T.y[:, 0:256], T.YS[:, 0:256], ["YS0"], ["y0"])
+    for w in range(4):
+        join(R - 1, 1, w)
+    quant_x(R, 1)
+    mm(7, 192, T.QV[:, :], T.QVS[:, :], T.QX[:, 256:448], T.QXS[:, 256:448], ["QV", "QXh1"])
+    for k in range(4):
+        dma("s" if k % 2 else "y", "sto%d" % (5 + k), T.osc[4 * k:4 * k + 4, :], T.QXS[32 * k:32 * k + 4, 0:448], ["QXh0", "QXh1"], ["osc%d" % k])
+    dma("y", "sto3", T.oc[:, 1024:1792], T.QX[:, 256:448].bitcast(dt.uint8), ["QXh1"], ["oc1"])
+    vcopy(T.YS[:, 256:448], T.PS[:, 3584:3776], ["bk7"], ["YS1"])
+    dma("s", "sto4", T.y[:, 256:448], T.YS[:, 256:448], ["YS1"], ["y1"])
+    kn = known["g"]
+    for s in sorted(cnt):
+        if kn.get(s, 0) < cnt[s]:
+            g.wait_ge(T.sem[s], cnt[s])

@@ -2,47 +2,40 @@ from concourse.mybir import dt, AluOpType as A, ActivationFunctionType as F
 
 C, R, N = 448, 3, 4
 H = [(0, 256), (256, 448)]
+HZ = [(0, 224), (224, 448)]
 BIG = -1.0e29
+NIL = 448
 
+
+def _b(n, t="float32"):
+    return ("sbuf", [128, n], t)
+
+
+BF, CODE, U8, U16, I32 = "bfloat16", "float8_e4m3fn_x4", "uint8", "uint16", "int32"
 SCRATCH = {
     "PS": ("psum", [128, 4096], "float32"),
-    "UT": ("sbuf", [128, 512], "bfloat16"), "VT": ("sbuf", [128, 512], "bfloat16"), "ZT": ("sbuf", [128, 512], "bfloat16"),
-    "QU": ("sbuf", [128, 128], "float8_e4m3fn_x4"), "QUS": ("sbuf", [128, 128], "uint8"),
-    "QU1": ("sbuf", [128, 128], "float8_e4m3fn_x4"), "QU1S": ("sbuf", [128, 128], "uint8"),
-    "QV": ("sbuf", [128, 128], "float8_e4m3fn_x4"), "QVS": ("sbuf", [128, 128], "uint8"),
-    "WC": ("sbuf", [128, 512], "float8_e4m3fn_x4"), "WS": ("sbuf", [128, 512], "uint8"),
-    "QX": ("sbuf", [128, 512], "float8_e4m3fn_x4"), "QXS": ("sbuf", [128, 512], "uint8"),
-    "PI": ("sbuf", [128, 28], "int32"), "PIX": ("sbuf", [128, 1], "int32"), "PMI": ("sbuf", [128, 1], "int32"), "GI": ("sbuf", [128, 1], "int32"),
-    "PM": ("sbuf", [128, 1], "float32"), "PF": ("sbuf", [128, 1], "float32"), "NG": ("sbuf", [128, 1], "float32"), "NG16": ("sbuf", [128, 1], "float32"),
-    "IO": ("sbuf", [128, 448], "float32"), "MD": ("sbuf", [128, 448], "float32"), "MASK": ("sbuf", [128, 448], "float32"),
-    "A16": ("sbuf", [128, 28], "float32"), "DB": ("sbuf", [128, 4], "float32"), "DUPL": ("sbuf", [128, 4], "uint16"),
-    "U1L": ("sbuf", [128, 8], "uint16"), "THR": ("sbuf", [128, 128], "bfloat16"),
-    "Z8": ("sbuf", [128, 8], "float32"), "JW": ("sbuf", [128, 28], "float32"), "PW": ("sbuf", [128, 28], "float32"), "JP": ("sbuf", [128, 28], "float32"),
-    "D16": ("sbuf", [128, 28], "uint16"), "NS": ("sbuf", [128, 4], "float32"),
-    "RUN": ("sbuf", [128, 32], "float32"), "LJ": ("sbuf", [128, 32], "float32"), "LV": ("sbuf", [128, 4], "float32"), "CF": ("sbuf", [128, 4], "float32"),
-    "SG": ("sbuf", [128, 1792], "bfloat16"), "CM": ("sbuf", [128, 1792], "bfloat16"), "SCN": ("sbuf", [128, 1792], "bfloat16"),
-    "NAT": ("sbuf", [128, 32], "float32"), "TT": ("sbuf", [128, 32], "float32"), "LT": ("sbuf", [128, 64], "float32"), "L2": ("sbuf", [128, 64], "float32"),
-    "LR": ("sbuf", [128, 64], "float32"), "RK": ("sbuf", [128, 28], "uint16"), "RK1": ("sbuf", [128, 28], "uint16"),
-    "PD": ("sbuf", [128, 456], "float32"), "RM": ("sbuf", [128, 448], "float32"), "SC": ("sbuf", [128, 232], "float32"),
-    "a1": ("sbuf", [128, 28], "float32"), "al": ("sbuf", [128, 28], "float32"), "b1": ("sbuf", [128, 28], "float32"),
-    "a2": ("sbuf", [128, 28], "float32"), "b2": ("sbuf", [128, 28], "float32"),
-    "m1": ("sbuf", [128, 28], "float32"), "m2": ("sbuf", [128, 28], "float32"), "m3": ("sbuf", [128, 28], "float32"),
-    "k1": ("sbuf", [128, 28], "float32"), "k2": ("sbuf", [128, 28], "float32"), "k3": ("sbuf", [128, 28], "float32"),
-    "dc": ("sbuf", [128, 28], "float32"), "u1": ("sbuf", [128, 28], "float32"), "ED": ("sbuf", [128, 28], "float32"), "EL": ("sbuf", [128, 28], "uint16"),
-    "JD": ("sbuf", [128, 28], "float32"), "PDF": ("sbuf", [128, 28], "float32"), "KK": ("sbuf", [128, 28], "float32"),
-    "Z": ("sbuf", [128, 1792], "bfloat16"), "YS": ("sbuf", [128, 448], "float32"),
+    "UT": _b(512, BF), "VT": _b(512, BF), "ZT": _b(512, BF), "Z": _b(1792, BF), "THR": _b(128, BF),
+    "SG": _b(1792, BF), "CM": _b(1792, BF), "SCN": _b(1792, BF),
+    "QU": _b(128, CODE), "QUS": _b(128, U8), "QU1": _b(128, CODE), "QU1S": _b(128, U8), "QV": _b(128, CODE), "QVS": _b(128, U8),
+    "WC": _b(512, CODE), "WS": _b(512, U8), "QX": _b(512, CODE), "QXS": _b(512, U8),
+    "PI": _b(28, I32), "PIX": _b(1, I32), "PMI": _b(1, I32), "GI": _b(1, I32),
+    "DUP0": _b(2, U16), "DUP1": _b(2, U16), "U1L": _b(8, U16),
+    "PM": _b(1), "PF": _b(1), "NG": _b(1), "NG16": _b(1), "GQ": _b(1), "WQ": _b(1), "PD": _b(456), "IO4": _b(1792), "MD": _b(448), "MASK": _b(448),
+    "A16": _b(28), "Z8": _b(8), "NS": _b(4), "RUN": _b(32), "LJ": _b(32), "LV": _b(4), "CF": _b(4),
+    "NAT": _b(32), "TT": _b(32), "LT0": _b(32), "LT1": _b(32), "LR": _b(64), "RM": _b(448), "SC": _b(232), "SCa": _b(120), "SCb": _b(120), "YS": _b(448),
 }
+for _i in ("EL", "RK", "RK1", "OL", "OF0", "OF1", "OF2", "OF3"):
+    SCRATCH[_i] = _b(28, U16)
+for _i in ("JW", "PW", "JP", "JD", "PDF", "KK", "Q", "wf", "lm", "mq", "a1", "a2", "al", "b1", "b2", "m1", "m2", "m3", "k1", "k2", "k3", "dc", "ED", "D1", "D2", "D3"):
+    SCRATCH[_i] = _b(28)
 for _i in range(4):
-    SCRATCH["X%d" % _i] = ("sbuf", [128, 1792], "bfloat16")
-    SCRATCH["DR%d" % _i] = ("sbuf", [128, 448], "float32")
-    SCRATCH["D%d" % _i] = ("sbuf", [128, 28], "float32")
-    SCRATCH["OF%d" % _i] = ("sbuf", [128, 28], "uint16")
-    SCRATCH["HS%d" % _i] = ("sbuf", [128, 448], "float32")
+    SCRATCH["X%d" % _i] = _b(1792, BF)
+    SCRATCH["HS%d" % _i] = _b(448)
+    SCRATCH["DR%d" % _i] = _b(448)
 for _i in range(R):
-    SCRATCH["QZ%d" % _i] = ("sbuf", [128, 448], "float8_e4m3fn_x4")
-    SCRATCH["QZS%d" % _i] = ("sbuf", [128, 448], "uint8")
-    SCRATCH["LZ%d" % _i] = ("sbuf", [128, 448], "float8_e4m3fn_x4")
-    SCRATCH["LS%d" % _i] = ("sbuf", [128, 448], "uint8")
+    for _n in ("QZ", "LZ"):
+        SCRATCH["%s%d" % (_n, _i)] = _b(448, CODE)
+        SCRATCH["%sS%d" % (_n, _i)] = _b(448, U8)
 
 SEMAPHORES = ["sv", "ss", "st", "sg", "loc"]
 SEMAPHORES += ["ld%d" % _i for _i in range(8)] + ["sto%d" % _i for _i in range(12)]
@@ -129,6 +122,10 @@ def rank_program(g, core, T, topo):
     def fill(ap, c, key):
         do("v", V.memset, (ap, c), [], [key])
 
+    def iota(out, pattern, key, mult=0, flag=True):
+        kw = {"allow_small_or_imprecise_dtypes": True} if flag else {}
+        do("g", g.iota, (out, pattern, 0, mult), [], [key], **kw)
+
     dma("y", "ld0", T.X0[:, 0:1024], T.x[:, 0:1024], [], ["X0h0"])
     dma("s", "ld1", T.UT[:, :], T.u[:, :], [], ["UT"])
     dma("s", "ld2", T.PI[:, :], T.p[:, :], [], ["PI"])
@@ -137,30 +134,34 @@ def rank_program(g, core, T, topo):
     dma("y", "ld5", T.WS[:, :], T.ws[:, :], [], ["WS"])
     dma("y", "ld6", T.VT[:, :], T.v[:, :], [], ["VT"])
 
-    do("g", g.iota, (T.PIX[:, :], [[0, 1]], 0, 1), [], ["PIX"])
-    do("g", g.iota, (T.DB[:, :], [[16, 2], [0, 2]], 0, 0), [], ["DB"], allow_small_or_imprecise_dtypes=True)
-    do("g", g.iota, (T.A16[:, :], [[16, 28]], 0, 0), [], ["A16"], allow_small_or_imprecise_dtypes=True)
-    do("g", g.iota, (T.IO[:, :], [[1, 448]], 0, 0), [], ["IO"], allow_small_or_imprecise_dtypes=True)
-    do("g", g.iota, (T.MD[:, :], [[0, 28], [1, 16]], 0, 0), [], ["MD"], allow_small_or_imprecise_dtypes=True)
+    iota(T.PIX[:, :], [[0, 1]], "PIX", 1, False)
+    iota(T.A16[:, :], [[16, 28]], "A16")
+    iota(T.MD[:, :], [[0, 28], [1, 16]], "MD")
+    iota(T.IO4[:, :], [[1, 448], [0, 4]], "IO4")
     fill(T.U1L[:, :], 1, "U1L")
     fill(T.ZT[:, :], 0.0, "ZT")
     fill(T.Z8[:, :], 0.0, "Z8")
     fill(T.SC[:, :], 0.0, "SC")
-    fill(T.PD[:, :], 0.0, "PD")
+    fill(T.SCa[:, :], 0.0, "SCa")
+    fill(T.SCb[:, :], 0.0, "SCb")
+    fill(T.PD[:, NIL:456], 0.0, "PDz")
     fill(T.TT[:, :], 0.0, "TT")
     quant(T.QX[:, 384:512], T.QXS[:, 384:512], T.ZT[:, :], ["ZT"], ["QXh1", "QXz"])
     ts(T.PMI[:, :], T.PIX[:, :], 15, None, [A.bitwise_and], ["PIX"], ["PMI"])
     ts(T.GI[:, :], T.PIX[:, :], 4, None, [A.arith_shift_right], ["PIX"], ["GI"])
     vcopy(T.PF[:, :], T.PIX[:, :], ["PIX"], ["PF"])
     vcopy(T.PM[:, :], T.PMI[:, :], ["PMI"], ["PM"])
-    ts(T.NG[:, :], T.GI[:, :], -1.0, None, [A.mult], ["GI"], ["NG"])
-    ts(T.NG16[:, :], T.GI[:, :], -1.0, -16.0, [A.mult, A.add], ["GI"], ["NG16"])
-    ts(T.DUPL[:, :], T.DB[:, :], T.PM[:, 0:1], None, [A.add], ["DB", "PM"], ["DUPL"])
+    ts(T.NG[:, :], T.GI[:, :], -1.0, -225.0, [A.mult, A.add], ["GI"], ["NG"])
+    ts(T.NG16[:, :], T.GI[:, :], -1.0, -241.0, [A.mult, A.add], ["GI"], ["NG16"])
+    ts(T.GQ[:, :], T.GI[:, :], 448.0, 448.0 * 242, [A.mult, A.add], ["GI"], ["GQ"])
+    fill(T.WQ[:, :], -448.0 * 447, "WQ")
+    for e in range(2):
+        ts(T["DUP%d" % e][:, :], T.Z8[:, 0:2], T.PM[:, 0:1], 16.0 * e, [A.add, A.add], ["Z8", "PM"], ["DUP%d" % e])
     ts(T.JW[:, :], T.A16[:, :], T.PM[:, 0:1], None, [A.add], ["A16", "PM"], ["JW"])
 
     quant(T.QU[:, :], T.QUS[:, :], T.UT[:, :], ["UT"], ["QU"])
     vcopy(T.QU1[:, :].bitcast(dt.uint32), T.QU[:, 0:128].bitcast(dt.uint32).indirect(T.U1L[:, 0:8]), ["QU", "U1L"], ["QU1c"])
-    vcopy(T.QU1S[:, :], T.QUS[:, 0:128].indirect(T.U1L[:, 0:8]), ["QU", "U1L"], ["QU1s"])
+    act(T.QU1S[:, :], T.QUS[:, 0:128].indirect(T.U1L[:, 0:8]), F.Copy, ["QU", "U1L"], ["QU1s"])
 
     def quant_x(t, h):
         a, b = H[h]
@@ -174,7 +175,7 @@ def rank_program(g, core, T, topo):
         mm(4 + h, b - a, T.QU1[:, :], T.QU1S[:, :], T.QX[:, a:b], T.QXS[:, a:b], ["QXh%d" % h, "QU1c", "QU1s"])
 
     def negs(m):
-        ts(T.NS[:, m:m + 1], T.PS[:, 512 * m + 1:512 * m + 2], -1.0, None, [A.mult], ["bk%d" % m], ["NS%d" % m])
+        act(T.NS[:, m:m + 1], T.PS[:, 512 * m + 1:512 * m + 2], F.Copy, ["bk%d" % m], ["NS%d" % m], scale=-1.0)
 
     def sign(m, h):
         a, b = H[h]
@@ -182,7 +183,7 @@ def rank_program(g, core, T, topo):
             ["bk%d" % (4 + h), "NS%d" % m], ["SG%d%d" % (m, h)], bias=T.NS[:, m:m + 1])
 
     def runmax(m):
-        scan(T.RUN[:, 8 * m:8 * m + 8], T.Z8[:, :], T.PS[:, 512 * m:512 * m + 128:16], BIG, A.add, A.max, ["Z8", "bk%d" % m], ["RUN%d" % m])
+        scan(T.RUN[:, 8 * m:8 * m + 8], T.Z8[:, :], T.PS[:, 512 * m:512 * m + 128:16], BIG, A.add, A.max, ["Z8", "bk%d" % m, "NS%d" % m], ["RUN%d" % m])
 
     def level(m):
         act(T.LJ[:, 8 * m:8 * m + 8], T.RUN[:, 8 * m:8 * m + 8], F.Sign, ["RUN%d" % m], ["LJ%d" % m, "LV%d" % m],
@@ -190,8 +191,7 @@ def rank_program(g, core, T, topo):
 
     def before(m, a, b, kind):
         o = 448 * m
-        hs = [h for h in (0, 1) if a < H[h][1] and b > H[h][0]]
-        rd = ["SG%d%d" % (m, h) for h in hs]
+        rd = ["SG%d%d" % (m, h) for h in (0, 1) if a < H[h][1] and b > H[h][0]]
         if kind == "tri":
             tt(T.CM[:, o + a:o + b], T.SG[:, o + a:o + b], T.THR[:, 0:b - a], A.is_gt, rd + ["THR"], ["CM%d.%d" % (m, a)])
         else:
@@ -202,193 +202,197 @@ def rank_program(g, core, T, topo):
         scan(T.SCN[:, 224 * m:224 * m + 224], T.CM[:, o:o + 224], T.CM[:, o + 224:o + 448], -225.0, A.add, A.add,
              ["CM%d.%d" % (m, a) for a in parts], ["SCN%d" % m])
 
-    def successor(src, dst):
-        vcopy(T.PD[:, 0:448].indirect(T.RK[:, 0:28]), src[0], ["RK", src[1]], ["PD"])
-        return dst
+    def vv(o, a, b, op):
+        tt(T[o][:, 0:28], T[a][:, 0:28], T[b][:, 0:28], op, (LRK if a == "LR" else [a]) + [b], [o])
 
-    def succ_gather():
-        vcopy(T.PD[:, 448:449], T.PD[:, 0:1], ["PD"], ["PD"])
-        tt(T.RM[:, :], T.PD[:, 0:456].indirect(T.RK1[:, 0:28]), T.MASK[:, :], A.mult, ["PD", "RK1", "MASK"], ["RM"])
+    def prep(t, o):
+        vv(o, {"JD": "JW", "PDF": "PW", "KK": "JP"}[o], "D%d" % t if t else "PW", A.subtract)
 
-    def succ_sum():
-        scan(T.SC[:, 1:225], T.RM[:, 0:448:2], T.RM[:, 1:448:2], 0.0, A.add, A.add, ["RM"], ["SC"])
-
-    def succ_diff(dst, key):
-        tt(dst, T.SC[:, 8:225:8], T.SC[:, 0:217:8], A.subtract, ["SC"], [key])
+    def scores_head():
+        negs(0); negs(1)
+        sign(0, 0); sign(1, 0)
 
     def scores_tail():
-        runmax(0); runmax(1)
-        negs(2); negs(3)
-        for m in (2, 3):
-            sign(m, 0)
         level(0); level(1)
-        before(0, 0, 128, "tri")
-        before(1, 0, 128, A.is_ge)
-        before(1, 128, 256, "tri")
-        runmax(2); runmax(3)
-        ts(T.CF[:, :], T.PS[:, 2:2048:512], 0.0, 16.0, [A.is_gt, A.mult], ["bk0", "bk1", "bk2", "bk3"], ["CF"])
+        negs(2); negs(3)
+        sign(2, 0); sign(3, 0)
         for m in range(4):
             sign(m, 1)
-            if m == 1:
-                level(2); level(3)
+        before(1, 0, 128, A.is_ge)
+        before(0, 0, 128, "tri")
+        before(1, 128, 256, "tri")
+        runmax(2); runmax(3)
+        level(2); level(3)
+        ts(T.CF[:, :], T.PS[:, 2:2048:512], 0.0, 16.0, [A.is_gt, A.mult], ["bk0", "bk1", "bk2", "bk3"], ["CF"])
         before(2, 0, 256, A.is_ge)
         before(3, 0, 256, A.is_ge)
         before(0, 128, 448, A.is_gt)
-        count(0, [0, 128])
         before(1, 256, 448, A.is_gt)
-        count(1, [0, 128, 256])
-        tt(T.SCN[:, 1119:1792:224], T.LV[:, :], T.CF[:, :], A.add, ["LV0", "LV1", "LV2", "LV3", "CF"], ["SCNw"])
+        count(0, [0, 128])
         before(2, 256, 384, "tri")
+        count(1, [0, 128, 256])
         before(2, 384, 448, A.is_gt)
-        count(2, [0, 256, 384])
-        before(3, 256, 384, A.is_ge)
         before(3, 384, 448, "tri")
+        before(3, 256, 384, A.is_ge)
+        count(2, [0, 256, 384])
         count(3, [0, 256, 384])
+        tt(T.SCN[:, 4 * 224 + 223:1792:224], T.LV[:, :], T.CF[:, :], A.add, ["LV0", "LV1", "LV2", "LV3", "CF"], ["SCNw"])
 
-    def wrapped():
+    LRK = ["LRe0", "LRe1", "LR1", "LR2", "LR3"]
+    RKK = ["RK%d" % b for b in range(4)]
+
+    def lists(t):
         rd = ["SCN0", "SCN1", "SCN2", "SCN3", "SCNw"]
+        prep(t, "JD")
         for b in range(4):
-            o, i = T.NAT[0:32, b:32:4], T.SCN[32 * b:32 * b + 32, 223:1792:224]
-            if b < 2:
-                vcopy(o, i, rd, ["NAT%d" % b])
-            else:
-                act(o, i, F.Copy, rd, ["NAT%d" % b])
-        do("v", V.transpose, (T.TT[0:32, 0:32], T.NAT[0:32, 0:32]), ["NAT0", "NAT1", "NAT2", "NAT3"], ["TT"])
-        vcopy(T.LT[:, :], T.TT[:, 0:32].indirect(T.DUPL[:, 0:4]), ["TT", "DUPL"], ["LT"])
-        do("v", V.transpose, (T.L2[0:32, 0:64], T.LT[0:32, 0:64]), ["LT"], ["L2"])
+            ts(T.NAT[0:32, b:32:4], T.SCN[32 * b:32 * b + 32, 223:1792:224], 225.0, None, [A.add], rd, ["NAT%d" % b])
+        prep(t, "PDF")
+        do("v", V.transpose, (T.TT[0:32, 0:32], T.NAT[0:32, 0:32]), ["NAT%d" % b for b in range(4)], ["TT"])
+        prep(t, "KK")
+        for e in range(2):
+            vcopy(T["LT%d" % e][:, :], T.TT[:, 0:32].indirect(T["DUP%d" % e][:, 0:2]), ["TT", "DUP%d" % e], ["LT%d" % e])
+        for e in range(2):
+            do("v", V.transpose, (T.LR[0:32, e:64:2], T["LT%d" % e][0:32, 0:32]), ["LT%d" % e], ["LRe%d" % e])
         for b in range(4):
-            vcopy(T.LR[32 * b:32 * b + 32, 0:64:2], T.L2[0:32, 0:32], ["L2"], ["LR0%d" % b])
-            act(T.LR[32 * b:32 * b + 32, 1:64:2], T.L2[0:32, 32:64], F.Copy, ["L2"], ["LR1%d" % b])
+            ts(T.RK[32 * b:32 * b + 32, :], T.LR[0:32, 0:28], -1.0, None, [A.add], ["LRe0", "LRe1"], ["RK%d" % b])
+        for b in range(1, 4):
+            act(T.LR[32 * b:32 * b + 32, 0:64], T.LR[0:32, 0:64], F.Copy, ["LRe0", "LRe1"], ["LR%d" % b])
 
-    LRK = ["LR%d%d" % (e, b) for e in range(2) for b in range(4)]
-
-    def prep(t):
-        d = T["D%d" % t][:, :] if t else T.PW[:, :]
-        k = "D%d" % t if t else "PW"
-        tt(T.JD[:, :], T.JW[:, :], d, A.subtract, ["JW", k], ["JD"])
-        tt(T.PDF[:, :], T.PW[:, :], d, A.subtract, ["PW", k], ["PDF"])
-        tt(T.KK[:, :], T.JP[:, :], d, A.subtract, ["JP", k], ["KK"])
+    def sorted_row(t):
+        vcopy(T.PD[:, 0:448].indirect(T.RK[:, 0:28]), T["DR%d" % t][:, :], RKK + ["DR%d" % t], ["PD"])
 
     def pointers(t):
-        d = T["D%d" % t][:, :] if t else T.PW[:, :]
         k = "D%d" % t if t else "PW"
         W = T.LR[:, 32:60]
-        ts(T.RK[:, :], T.LR[:, 0:28], 224.0, None, [A.add], LRK, ["RK"])
-        vcopy(T.PD[:, 0:448].indirect(T.RK[:, 0:28]), T["DR%d" % t][:, :], ["RK", "DR%d" % t], ["PD"])
+        sorted_row(t)
+        act(T.wf[:, :], T.LR[:, 0:28], F.Relu, LRK + ["WQ"], ["wf"], bias=T.WQ[:, 0:1], scale=448.0)
+        act(T.Q[:, :], W, F.Relu, LRK + ["GQ"], ["Q"], bias=T.GQ[:, 0:1], scale=-448.0)
         act(T.a1[:, :], W, F.Sign, LRK + ["NG16"], ["a1"], bias=T.NG16[:, 0:1])
         act(T.a2[:, :], W, F.Sign, LRK + ["NG"], ["a2"], bias=T.NG[:, 0:1])
         act(T.b1[:, :], T.a1[:, :], F.Square, ["a1"], ["b1"])
         act(T.b2[:, :], T.a2[:, :], F.Square, ["a2"], ["b2"])
         act(T.al[:, :], T.a1[:, :], F.Relu, ["a1"], ["al"])
-        ts(T.RK1[:, :], T.LR[:, 0:28], 225.0, None, [A.add], LRK, ["RK1"])
-        succ_gather()
-        tt(T.m1[:, :], T.b1[:, :], T.JD[:, :], A.mult, ["b1", "JD"], ["m1"])
-        tt(T.m2[:, :], T.b2[:, :], T.PDF[:, :], A.mult, ["b2", "PDF"], ["m2"])
-        tt(T.m3[:, :], T.al[:, :], d, A.mult, ["al", k], ["m3"])
-        succ_sum()
-        tt(T.k1[:, :], T.KK[:, :], T.m1[:, :], A.subtract, ["KK", "m1"], ["k1"])
-        tt(T.k2[:, :], T.m2[:, :], T.m3[:, :], A.add, ["m2", "m3"], ["k2"])
-        succ_diff(T.dc[:, :], "dc")
-        tt(T.k3[:, :], T.k1[:, :], T.k2[:, :], A.subtract, ["k1", "k2"], ["k3"])
-        tt(T.u1[:, :], T.al[:, :], T.dc[:, :], A.mult, ["al", "dc"], ["u1"])
+        vv("lm", "LR", "wf", A.subtract)
+        vv("m1", "b1", "JD", A.mult)
+        vv("mq", "lm", "Q", A.max)
+        vv("m2", "b2", "PDF", A.mult)
+        ts(T.OL[:, :], T.mq[:, :], float(NIL), None, [A.min], ["mq"], ["OL"])
+        vv("m3", "al", k, A.mult)
+        tt(T.RM[:, :], T.PD[:, 0:456].indirect(T.OL[:, 0:28]), T.MASK[:, :], A.mult, ["PD", "PDz", "OL", "MASK"], ["RM"])
+        vv("k1", "KK", "m1", A.subtract)
+        scan(T.SC[:, 1:225], T.RM[:, 0:448:2], T.RM[:, 1:448:2], 0.0, A.add, A.add, ["RM"], ["SC"])
+        vv("k2", "m2", "m3", A.add)
+        tt(T.dc[:, :], T.SC[:, 8:225:8], T.SC[:, 0:217:8], A.subtract, ["SC"], ["dc"])
+        vv("k3", "k1", "k2", A.subtract)
+        vcopy(T.RK1[:, :], T.lm[:, :], ["lm"], ["RK1"])
         n = "D%d" % (t + 1)
-        tt(T[n][:, :], T.u1[:, :], T.k3[:, :], A.add, ["u1", "k3"], [n])
+        vv(n, "dc", "k3", A.add)
         for e in (2, 0, 3, 1):
             ts(T["OF%d" % e][:, :], T[n][:, :], 4.0, float(e), [A.mult, A.add], [n], ["OF%d" % e])
 
     def send(t, h):
-        a, b = H[h]
+        a, b = HZ[h]
         dst = T.cores[(rank + 1 + t) % N]
         rid, pid, _ = topo.addr(dst)
         m = topo.mask(core, dst)
         waits("g", ["QZ%dh%d" % (t, h)], [])
         g.remote_dma(T["LZ%d" % t][:, a:b].bitcast(dt.uint8), T["QZ%d" % t][:, a:b].bitcast(dt.uint8),
                      T.sem["ar%d%dc" % (t, h)], T.sem.loc, pid, rid, m)
-        g.remote_dma(T["LS%d" % t][:, a:b], T["QZS%d" % t][:, a:b], T.sem["ar%d%ds" % (t, h)], T.sem.loc, pid, rid, m)
-        e = len(topo.engines(core, dst))
-        cnt["loc"] = cnt.get("loc", 0) + 2 * e
-        src = T.cores[(rank - 1 - t) % N]
-        e = len(topo.engines(src, core))
+        g.remote_dma(T["LZS%d" % t][:, a:b], T["QZS%d" % t][:, a:b], T.sem["ar%d%ds" % (t, h)], T.sem.loc, pid, rid, m)
+        cnt["loc"] = cnt.get("loc", 0) + 2 * len(topo.engines(core, dst))
+        e = len(topo.engines(T.cores[(rank - 1 - t) % N], core))
         lastw["LZ%dh%d" % (t, h)] = ("ar%d%dc" % (t, h), e, None)
-        lastw["LS%dh%d" % (t, h)] = ("ar%d%ds" % (t, h), e, None)
+        lastw["LZS%dh%d" % (t, h)] = ("ar%d%ds" % (t, h), e, None)
 
     def mosaic(t):
         X = T["X%d" % t]
-        xk = ["X%dh0" % t, "X%dh1" % t]
-        n = "D%d" % (t + 1)
-        for h in range(2):
-            a, b = H[h]
-            for e in (2, 3):
-                act(T.Z[:, 4 * a + e:4 * b:4], X[:, 0:1792].indirect(T["OF%d" % e][:, a // 16:b // 16]), F.Copy,
-                    xk + ["OF%d" % e], ["Zh%d.%d" % (h, e)])
-            for e in (0, 1):
-                vcopy(T.Z[:, 4 * a + e:4 * b:4], X[:, 0:1792].indirect(T["OF%d" % e][:, a // 16:b // 16]),
-                      xk + ["OF%d" % e], ["Zh%d.%d" % (h, e)])
+
+        def part(h, e):
+            a, b = HZ[h]
+            o, i = T.Z[:, 4 * a + e:4 * b:4], X[:, 0:1792].indirect(T["OF%d" % e][:, a // 16:b // 16])
+            rd, wr = ["X%dh0" % t, "X%dh1" % t, "OF%d" % e], ["Zh%d.%d" % (h, e)]
+            if e >= 2:
+                act(o, i, F.Copy, rd, wr)
+            else:
+                vcopy(o, i, rd, wr)
+
+        def pack(h):
+            a, b = HZ[h]
             quant(T["QZ%d" % t][:, a:b], T["QZS%d" % t][:, a:b], T.Z[:, 4 * a:4 * b],
                   ["Zh%d.%d" % (h, e) for e in range(4)], ["QZ%dh%d" % (t, h)])
             send(t, h)
-            if h == 0:
-                vcopy(T.D16[:, :], T[n][:, :], [n], ["D16"])
-        act(T["DR%d" % (t + 1)][:, :], T.IO[:, 0:448].indirect(T.D16[:, 0:28]), F.Copy, ["IO", "D16"], ["DR%d" % (t + 1)])
+
+        for h in range(2):
+            part(h, 2); part(h, 3)
+        for h in range(2):
+            part(h, 0); part(h, 1)
+            pack(h)
+        act(T["DR%d" % (t + 1)][:, :], T.IO4[:, :].indirect(T.OF0[:, 0:28]), F.Copy, ["IO4", "OF0"], ["DR%d" % (t + 1)])
 
     def join_list(t):
-        if t < R - 1:
-            prep(t + 1)
-        vcopy(T.PD[:, 0:448].indirect(T.RK[:, 0:28]), T["DR%d" % (t + 1)][:, :], ["RK", "DR%d" % (t + 1)], ["PD"])
-        succ_gather()
-        succ_sum()
-        succ_diff(T.ED[:, :], "ED")
-        vcopy(T.EL[:, :], T.ED[:, :], ["ED"], ["EL"])
+        sorted_row(t + 1)
+        for h, s in enumerate("ab"):
+            tt(T.RM[:, 224 * h:224 * h + 224], T.PD[:, 0:456].indirect(T.RK1[:, 14 * h:14 * h + 14]), T.MASK[:, 224 * h:224 * h + 224], A.mult,
+               ["PD", "PDz", "RK1", "MASK", "RM"], ["RM" + s])
+        for h, s in enumerate("ab"):
+            o = 224 * h
+            scan(T["SC" + s][:, 1:113], T.RM[:, o:o + 224:2], T.RM[:, o + 1:o + 224:2], 0.0, A.add, A.add, ["RM" + s], ["SC" + s])
+        for h, s in enumerate("ab"):
+            tt(T.ED[:, 14 * h:14 * h + 14], T["SC" + s][:, 8:113:8], T["SC" + s][:, 0:105:8], A.subtract, ["SC" + s], ["ED" + s])
+        for h, s in enumerate("ab"):
+            vcopy(T.EL[:, 14 * h:14 * h + 14], T.ED[:, 14 * h:14 * h + 14], ["ED" + s], ["EL" + s])
 
     def layer(t):
         for h in range(2):
-            a, b = H[h]
+            a, b = HZ[h]
             for w in range(4):
-                mm(2 * w + h, b - a, T.WC[:, 128 * w:128 * w + 128], T.WS[:, 128 * w:128 * w + 128], T["LZ%d" % t][:, a:b], T["LS%d" % t][:, a:b],
-                   ["WC", "WS", "LZ%dh%d" % (t, h), "LS%dh%d" % (t, h)])
-                bk = 2 * w + h
-                act(T["HS%d" % w][:, a:b], T.PS[:, 512 * bk:512 * bk + b - a], F.Copy, ["bk%d" % bk], ["HS%dh%d" % (w, h)], scale=0.00390625)
+                mm(2 * w + h, b - a, T.WC[:, 128 * w:128 * w + 128], T.WS[:, 128 * w:128 * w + 128], T["LZ%d" % t][:, a:b], T["LZS%d" % t][:, a:b],
+                   ["WC", "WS", "LZ%dh%d" % (t, h), "LZS%dh%d" % (t, h)])
+        for w, h in ((0, 0), (1, 0), (0, 1), (2, 0), (1, 1), (3, 0), (2, 1), (3, 1)):
+            a, b = HZ[h]
+            bk = 2 * w + h
+            act(T["HS%d" % w][:, a:b], T.PS[:, 512 * bk:512 * bk + b - a], F.Copy, ["bk%d" % bk], ["HS%dh%d" % (w, h)], scale=0.00390625)
 
-    def join(t, h, w):
+    def join(t, h, ws=range(4)):
         a, b = H[h]
-        tt(T["X%d" % (t + 1)][:, 4 * a + w:4 * b:4], T["HS%d" % w][:, 0:448].indirect(T.EL[:, a // 16:b // 16]),
-           T["X%d" % t][:, 4 * a + w:4 * b:4], A.add, ["HS%dh0" % w, "HS%dh1" % w, "EL", "X%dh%d" % (t, h)], ["X%dh%d.%d" % (t + 1, h, w)])
-        if w == 3:
-            lastw["X%dh%d" % (t + 1, h)] = lastw["X%dh%d.3" % (t + 1, h)]
+        for w in ws:
+            tt(T["X%d" % (t + 1)][:, 4 * a + w:4 * b:4], T["HS%d" % w][:, 0:448].indirect(T.EL[:, a // 16:b // 16]),
+               T["X%d" % t][:, 4 * a + w:4 * b:4], A.add, ["HS%dh0" % w, "HS%dh1" % w, "ELa", "ELb", "X%dh%d" % (t, h)], ["X%dh%d.%d" % (t + 1, h, w)])
+        lastw["X%dh%d" % (t + 1, h)] = lastw["X%dh%d.%d" % (t + 1, h, ws[-1])]
 
     quant_x(0, 0)
     products(0)
-    ts(T.THR[:, :], T.IO[:, 0:128], T.PF[:, 0:1], 0.5, [A.is_gt, A.subtract], ["IO", "PF"], ["THR"])
-    negs(0); negs(1)
-    sign(0, 0); sign(1, 0)
+    scores_head()
     quant_x(0, 1)
     products(1)
     vcopy(T.PW[:, :], T.PI[:, :], ["PI"], ["PW"])
-    vcopy(T.D16[:, :], T.PI[:, :], ["PI"], ["D16"])
-    scores_tail()
-    act(T.DR0[:, :], T.IO[:, 0:448].indirect(T.D16[:, 0:28]), F.Copy, ["IO", "D16"], ["DR0"])
-    tt(T.JP[:, :], T.JW[:, :], T.PW[:, :], A.add, ["JW", "PW"], ["JP"])
-    prep(0)
+    ts(T.OF0[:, :], T.PI[:, :], 4.0, None, [A.mult], ["PI"], ["OF0"])
+    runmax(0); runmax(1)
     ts(T.MASK[:, :], T.MD[:, :], T.PM[:, 0:1], None, [A.is_equal], ["MD", "PM"], ["MASK"])
+    vv("JP", "JW", "PW", A.add)
+    ts(T.THR[:, :], T.IO4[:, 0:512:4], T.PF[:, 0:1], 0.5, [A.is_gt, A.subtract], ["IO4", "PF"], ["THR"])
+    scores_tail()
+    act(T.DR0[:, :], T.IO4[:, :].indirect(T.OF0[:, 0:28]), F.Copy, ["IO4", "OF0"], ["DR0"])
 
     for t in range(R):
-        wrapped()
+        lists(t)
         pointers(t)
         mosaic(t)
         join_list(t)
         layer(t)
         if t == 0:
             quant(T.QV[:, :], T.QVS[:, :], T.VT[:, :], ["VT"], ["QV"])
-        for w in range(4):
-            join(t, 0, w)
+        join(t, 0)
+        if t < R - 1:
+            join(t, 1, [0])
         quant_x(t + 1, 0)
         if t < R - 1:
             products(0)
-            join(t, 1, 0)
-            negs(0); negs(1)
-            sign(0, 0); sign(1, 0)
-            for w in (1, 2, 3):
-                join(t, 1, w)
+            scores_head()
+            join(t, 1, [1, 2])
+            runmax(0)
+            join(t, 1, [3])
+            runmax(1)
             quant_x(t + 1, 1)
             products(1)
             scores_tail()
@@ -397,13 +401,12 @@ def rank_program(g, core, T, topo):
     mm(6, 256, T.QV[:, :], T.QVS[:, :], T.QX[:, 0:256], T.QXS[:, 0:256], ["QV", "QXh0"])
     act(T.YS[:, 0:256], T.PS[:, 3072:3328], F.Copy, ["bk6"], ["YS0"])
     dma("y", "sto2", T.y[:, 0:256], T.YS[:, 0:256], ["YS0"], ["y0"])
-    for w in range(4):
-        join(R - 1, 1, w)
+    join(R - 1, 1)
     quant_x(R, 1)
     mm(7, 192, T.QV[:, :], T.QVS[:, :], T.QX[:, 256:448], T.QXS[:, 256:448], ["QV", "QXh1"])
+    dma("y", "sto3", T.oc[:, 1024:1792], T.QX[:, 256:448].bitcast(dt.uint8), ["QXh1"], ["oc1"])
     for k in range(4):
         dma("s" if k % 2 else "y", "sto%d" % (5 + k), T.osc[4 * k:4 * k + 4, :], T.QXS[32 * k:32 * k + 4, 0:448], ["QXh0", "QXh1"], ["osc%d" % k])
-    dma("y", "sto3", T.oc[:, 1024:1792], T.QX[:, 256:448].bitcast(dt.uint8), ["QXh1"], ["oc1"])
     vcopy(T.YS[:, 256:448], T.PS[:, 3584:3776], ["bk7"], ["YS1"])
     dma("s", "sto4", T.y[:, 256:448], T.YS[:, 256:448], ["YS1"], ["y1"])
     kn = known["g"]

from concourse.mybir import dt, AluOpType as A, ActivationFunctionType as F

C, R, N = 448, 3, 4
H = [(0, 256), (256, 448)]
HZ = [(0, 224), (224, 448)]
BIG = -1.0e29
NIL = 448


def _b(n, t="float32"):
    return ("sbuf", [128, n], t)


BF, CODE, U8, U16, I32 = "bfloat16", "float8_e4m3fn_x4", "uint8", "uint16", "int32"
SCRATCH = {
    "PS": ("psum", [128, 4096], "float32"),
    "UT": _b(512, BF), "VT": _b(512, BF), "ZT": _b(512, BF), "Z": _b(1792, BF), "THR": _b(128, BF),
    "SG": _b(1792, BF), "CM": _b(1792, BF), "SCN": _b(1792, BF),
    "QU": _b(128, CODE), "QUS": _b(128, U8), "QU1": _b(128, CODE), "QU1S": _b(128, U8), "QV": _b(128, CODE), "QVS": _b(128, U8),
    "WC": _b(512, CODE), "WS": _b(512, U8), "QX": _b(512, CODE), "QXS": _b(512, U8),
    "PI": _b(28, I32), "PIX": _b(1, I32), "PMI": _b(1, I32), "GI": _b(1, I32),
    "DUP0": _b(2, U16), "DUP1": _b(2, U16), "U1L": _b(8, U16),
    "PM": _b(1), "PF": _b(1), "NG": _b(1), "NG16": _b(1), "GQ": _b(1), "WQ": _b(1), "PD": _b(456), "IO4": _b(1792), "MD": _b(448), "MASK": _b(448),
    "A16": _b(28), "Z8": _b(8), "NS": _b(4), "RUN": _b(32), "LJ": _b(32), "LV": _b(4), "CF": _b(4),
    "NAT": _b(32), "TT": _b(32), "LT0": _b(32), "LT1": _b(32), "LR": _b(64), "RM": _b(448), "SC": _b(232), "SCa": _b(120), "SCb": _b(120), "YS": _b(448),
}
for _i in ("EL", "RK", "RK1", "OL", "OF0", "OF1", "OF2", "OF3"):
    SCRATCH[_i] = _b(28, U16)
for _i in ("JW", "PW", "JP", "JD", "PDF", "KK", "Q", "wf", "lm", "mq", "a1", "a2", "al", "b1", "b2", "m1", "m2", "m3", "k1", "k2", "k3", "dc", "ED", "D1", "D2", "D3"):
    SCRATCH[_i] = _b(28)
for _i in range(4):
    SCRATCH["X%d" % _i] = _b(1792, BF)
    SCRATCH["HS%d" % _i] = _b(448)
    SCRATCH["DR%d" % _i] = _b(448)
for _i in range(R):
    for _n in ("QZ", "LZ"):
        SCRATCH["%s%d" % (_n, _i)] = _b(448, CODE)
        SCRATCH["%sS%d" % (_n, _i)] = _b(448, U8)

SEMAPHORES = ["sv", "ss", "st", "sg", "loc"]
SEMAPHORES += ["ld%d" % _i for _i in range(8)] + ["sto%d" % _i for _i in range(12)]
SEMAPHORES += ["ar%d%d%s" % (_t, _h, _k) for _t in range(R) for _h in range(2) for _k in "cs"]


def rank_program(g, core, T, topo):
    rank = T.rank_of(core)
    if rank is None:
        return
    q = {"v": g.vector, "s": g.scalar, "t": g.tensor, "g": g, "y": g.sync}
    own = {"v": "sv", "s": "ss", "t": "st", "g": "sg"}
    cnt, known, clock, lastw, readers = {}, {k: {} for k in q}, {}, {}, {}

    def waits(qn, reads, writes):
        need = {}
        for k in reads:
            if k in lastw:
                s, n, _ = lastw[k]
                need[s] = max(need.get(s, 0), n)
        for k in writes:
            if k in lastw:
                s, n, _ = lastw[k]
                need[s] = max(need.get(s, 0), n)
            for s, n, rq in readers.get(k, []):
                if rq != qn:
                    need[s] = max(need.get(s, 0), n)
        kn = known[qn]
        need = {s: n for s, n in need.items() if kn.get(s, 0) < n}
        for s in list(need):
            if any(o != s and clock.get((o, need[o]), {}).get(s, 0) >= need[s] for o in need):
                del need[s]
        for s, n in need.items():
            q[qn].wait_ge(T.sem[s], n)
            for o, m in clock.get((s, n), {}).items():
                kn[o] = max(kn.get(o, 0), m)
            kn[s] = max(kn.get(s, 0), n)

    def note(qn, reads, writes, s, n, dma):
        clock[(s, n)] = dict(known[qn])
        for k in writes:
            lastw[k] = (s, n, qn)
            readers[k] = []
        for k in reads:
            readers.setdefault(k, []).append((s, n, None if dma else qn))

    def do(qn, fn, args, reads, writes, **kw):
        waits(qn, reads, writes)
        s = own[qn]
        n = cnt.get(s, 0) + 1
        cnt[s] = n
        fn(*args, **kw).then_inc(T.sem[s], 1)
        note(qn, reads, writes, s, n, False)

    def dma(qn, s, out, in_, reads, writes):
        waits(qn, reads, writes)
        q[qn].dma_start(out, in_).then_inc(T.sem[s], 16)
        cnt[s] = 16
        note(qn, reads, writes, s, 16, True)

    V, S, TE = g.vector, g.scalar, g.tensor

    def ts(out, in0, s1, s2, ops, reads, writes):
        do("v", V.tensor_scalar, (out, in0, s1, s2) + tuple(ops), reads, writes)

    def tt(out, a, b, op, reads, writes):
        do("v", V.tensor_tensor, (out, a, b, op), reads, writes)

    def vcopy(out, a, reads, writes):
        do("v", V.tensor_copy, (out, a), reads, writes)

    def act(out, a, f, reads, writes, **kw):
        do("s", S.activation, (out, a, f), reads, writes, **kw)

    def scan(out, a, b, init, o0, o1, reads, writes):
        do("v", V.tensor_tensor_scan, (out, a, b, init, o0, o1), reads, writes)

    def quant(oc, os_, tile, reads, writes):
        do("v", V.quantize_mx, (oc, os_, tile), reads, writes)

    def mm(bank, n, l, ls, r, rs, reads):
        do("t", TE.matmul_mx, (T.PS[:, 512 * bank:512 * bank + n], l, ls, r, rs, True, True), reads, ["bk%d" % bank])

    def fill(ap, c, key):
        do("v", V.memset, (ap, c), [], [key])

    def iota(out, pattern, key, mult=0, flag=True):
        kw = {"allow_small_or_imprecise_dtypes": True} if flag else {}
        do("g", g.iota, (out, pattern, 0, mult), [], [key], **kw)

    dma("y", "ld0", T.X0[:, 0:1024], T.x[:, 0:1024], [], ["X0h0"])
    dma("s", "ld1", T.UT[:, :], T.u[:, :], [], ["UT"])
    dma("s", "ld2", T.PI[:, :], T.p[:, :], [], ["PI"])
    dma("y", "ld3", T.X0[:, 1024:1792], T.x[:, 1024:1792], [], ["X0h1"])
    dma("y", "ld4", T.WC[:, :].bitcast(dt.uint8), T.wc[:, :], [], ["WC"])
    dma("y", "ld5", T.WS[:, :], T.ws[:, :], [], ["WS"])
    dma("y", "ld6", T.VT[:, :], T.v[:, :], [], ["VT"])

    iota(T.PIX[:, :], [[0, 1]], "PIX", 1, False)
    iota(T.A16[:, :], [[16, 28]], "A16")
    iota(T.MD[:, :], [[0, 28], [1, 16]], "MD")
    iota(T.IO4[:, :], [[1, 448], [0, 4]], "IO4")
    fill(T.U1L[:, :], 1, "U1L")
    fill(T.ZT[:, :], 0.0, "ZT")
    fill(T.Z8[:, :], 0.0, "Z8")
    fill(T.SC[:, :], 0.0, "SC")
    fill(T.SCa[:, :], 0.0, "SCa")
    fill(T.SCb[:, :], 0.0, "SCb")
    fill(T.PD[:, NIL:456], 0.0, "PDz")
    fill(T.TT[:, :], 0.0, "TT")
    quant(T.QX[:, 384:512], T.QXS[:, 384:512], T.ZT[:, :], ["ZT"], ["QXh1", "QXz"])
    ts(T.PMI[:, :], T.PIX[:, :], 15, None, [A.bitwise_and], ["PIX"], ["PMI"])
    ts(T.GI[:, :], T.PIX[:, :], 4, None, [A.arith_shift_right], ["PIX"], ["GI"])
    vcopy(T.PF[:, :], T.PIX[:, :], ["PIX"], ["PF"])
    vcopy(T.PM[:, :], T.PMI[:, :], ["PMI"], ["PM"])
    ts(T.NG[:, :], T.GI[:, :], -1.0, -225.0, [A.mult, A.add], ["GI"], ["NG"])
    ts(T.NG16[:, :], T.GI[:, :], -1.0, -241.0, [A.mult, A.add], ["GI"], ["NG16"])
    ts(T.GQ[:, :], T.GI[:, :], 448.0, 448.0 * 242, [A.mult, A.add], ["GI"], ["GQ"])
    fill(T.WQ[:, :], -448.0 * 447, "WQ")
    for e in range(2):
        ts(T["DUP%d" % e][:, :], T.Z8[:, 0:2], T.PM[:, 0:1], 16.0 * e, [A.add, A.add], ["Z8", "PM"], ["DUP%d" % e])
    ts(T.JW[:, :], T.A16[:, :], T.PM[:, 0:1], None, [A.add], ["A16", "PM"], ["JW"])

    quant(T.QU[:, :], T.QUS[:, :], T.UT[:, :], ["UT"], ["QU"])
    vcopy(T.QU1[:, :].bitcast(dt.uint32), T.QU[:, 0:128].bitcast(dt.uint32).indirect(T.U1L[:, 0:8]), ["QU", "U1L"], ["QU1c"])
    act(T.QU1S[:, :], T.QUS[:, 0:128].indirect(T.U1L[:, 0:8]), F.Copy, ["QU", "U1L"], ["QU1s"])

    def quant_x(t, h):
        a, b = H[h]
        quant(T.QX[:, a:b], T.QXS[:, a:b], T["X%d" % t][:, 4 * a:4 * b], ["X%dh%d" % (t, h)], ["QXh%d" % h])

    def products(h):
        a, b = H[h]
        for m in (0, 1) if h == 0 else (2, 3):
            mm(m, 128, T.QX[:, 128 * m:128 * m + 128], T.QXS[:, 128 * m:128 * m + 128], T.QU[:, :], T.QUS[:, :],
               ["QXh%d" % h, "QU"] + (["QXz"] if m == 3 else []))
        mm(4 + h, b - a, T.QU1[:, :], T.QU1S[:, :], T.QX[:, a:b], T.QXS[:, a:b], ["QXh%d" % h, "QU1c", "QU1s"])

    def negs(m):
        act(T.NS[:, m:m + 1], T.PS[:, 512 * m + 1:512 * m + 2], F.Copy, ["bk%d" % m], ["NS%d" % m], scale=-1.0)

    def sign(m, h):
        a, b = H[h]
        act(T.SG[:, 448 * m + a:448 * m + b], T.PS[:, 512 * (4 + h):512 * (4 + h) + b - a], F.Sign,
            ["bk%d" % (4 + h), "NS%d" % m], ["SG%d%d" % (m, h)], bias=T.NS[:, m:m + 1])

    def runmax(m):
        scan(T.RUN[:, 8 * m:8 * m + 8], T.Z8[:, :], T.PS[:, 512 * m:512 * m + 128:16], BIG, A.add, A.max, ["Z8", "bk%d" % m, "NS%d" % m], ["RUN%d" % m])

    def level(m):
        act(T.LJ[:, 8 * m:8 * m + 8], T.RUN[:, 8 * m:8 * m + 8], F.Sign, ["RUN%d" % m], ["LJ%d" % m, "LV%d" % m],
            bias=T.RUN[:, 8 * m + 7:8 * m + 8], scale=-1.0, accum_out=T.LV[:, m:m + 1])

    def before(m, a, b, kind):
        o = 448 * m
        rd = ["SG%d%d" % (m, h) for h in (0, 1) if a < H[h][1] and b > H[h][0]]
        if kind == "tri":
            tt(T.CM[:, o + a:o + b], T.SG[:, o + a:o + b], T.THR[:, 0:b - a], A.is_gt, rd + ["THR"], ["CM%d.%d" % (m, a)])
        else:
            ts(T.CM[:, o + a:o + b], T.SG[:, o + a:o + b], 0.0, None, [kind], rd, ["CM%d.%d" % (m, a)])

    def count(m, parts):
        o = 448 * m
        scan(T.SCN[:, 224 * m:224 * m + 224], T.CM[:, o:o + 224], T.CM[:, o + 224:o + 448], -225.0, A.add, A.add,
             ["CM%d.%d" % (m, a) for a in parts], ["SCN%d" % m])

    def vv(o, a, b, op):
        tt(T[o][:, 0:28], T[a][:, 0:28], T[b][:, 0:28], op, (LRK if a == "LR" else [a]) + [b], [o])

    def prep(t, o):
        vv(o, {"JD": "JW", "PDF": "PW", "KK": "JP"}[o], "D%d" % t if t else "PW", A.subtract)

    def scores_head():
        negs(0); negs(1)
        sign(0, 0); sign(1, 0)

    def scores_tail():
        level(0); level(1)
        negs(2); negs(3)
        sign(2, 0); sign(3, 0)
        for m in range(4):
            sign(m, 1)
        before(1, 0, 128, A.is_ge)
        before(0, 0, 128, "tri")
        before(1, 128, 256, "tri")
        runmax(2); runmax(3)
        level(2); level(3)
        ts(T.CF[:, :], T.PS[:, 2:2048:512], 0.0, 16.0, [A.is_gt, A.mult], ["bk0", "bk1", "bk2", "bk3"], ["CF"])
        before(2, 0, 256, A.is_ge)
        before(3, 0, 256, A.is_ge)
        before(0, 128, 448, A.is_gt)
        before(1, 256, 448, A.is_gt)
        count(0, [0, 128])
        before(2, 256, 384, "tri")
        count(1, [0, 128, 256])
        before(2, 384, 448, A.is_gt)
        before(3, 384, 448, "tri")
        before(3, 256, 384, A.is_ge)
        count(2, [0, 256, 384])
        count(3, [0, 256, 384])
        tt(T.SCN[:, 4 * 224 + 223:1792:224], T.LV[:, :], T.CF[:, :], A.add, ["LV0", "LV1", "LV2", "LV3", "CF"], ["SCNw"])

    LRK = ["LRe0", "LRe1", "LR1", "LR2", "LR3"]
    RKK = ["RK%d" % b for b in range(4)]

    def lists(t):
        rd = ["SCN0", "SCN1", "SCN2", "SCN3", "SCNw"]
        prep(t, "JD")
        for b in range(4):
            ts(T.NAT[0:32, b:32:4], T.SCN[32 * b:32 * b + 32, 223:1792:224], 225.0, None, [A.add], rd, ["NAT%d" % b])
        prep(t, "PDF")
        do("v", V.transpose, (T.TT[0:32, 0:32], T.NAT[0:32, 0:32]), ["NAT%d" % b for b in range(4)], ["TT"])
        prep(t, "KK")
        for e in range(2):
            vcopy(T["LT%d" % e][:, :], T.TT[:, 0:32].indirect(T["DUP%d" % e][:, 0:2]), ["TT", "DUP%d" % e], ["LT%d" % e])
        for e in range(2):
            do("v", V.transpose, (T.LR[0:32, e:64:2], T["LT%d" % e][0:32, 0:32]), ["LT%d" % e], ["LRe%d" % e])
        for b in range(4):
            ts(T.RK[32 * b:32 * b + 32, :], T.LR[0:32, 0:28], -1.0, None, [A.add], ["LRe0", "LRe1"], ["RK%d" % b])
        for b in range(1, 4):
            act(T.LR[32 * b:32 * b + 32, 0:64], T.LR[0:32, 0:64], F.Copy, ["LRe0", "LRe1"], ["LR%d" % b])

    def sorted_row(t):
        vcopy(T.PD[:, 0:448].indirect(T.RK[:, 0:28]), T["DR%d" % t][:, :], RKK + ["DR%d" % t], ["PD"])

    def pointers(t):
        k = "D%d" % t if t else "PW"
        W = T.LR[:, 32:60]
        sorted_row(t)
        act(T.wf[:, :], T.LR[:, 0:28], F.Relu, LRK + ["WQ"], ["wf"], bias=T.WQ[:, 0:1], scale=448.0)
        act(T.Q[:, :], W, F.Relu, LRK + ["GQ"], ["Q"], bias=T.GQ[:, 0:1], scale=-448.0)
        act(T.a1[:, :], W, F.Sign, LRK + ["NG16"], ["a1"], bias=T.NG16[:, 0:1])
        act(T.a2[:, :], W, F.Sign, LRK + ["NG"], ["a2"], bias=T.NG[:, 0:1])
        act(T.b1[:, :], T.a1[:, :], F.Square, ["a1"], ["b1"])
        act(T.b2[:, :], T.a2[:, :], F.Square, ["a2"], ["b2"])
        act(T.al[:, :], T.a1[:, :], F.Relu, ["a1"], ["al"])
        vv("lm", "LR", "wf", A.subtract)
        vv("m1", "b1", "JD", A.mult)
        vv("mq", "lm", "Q", A.max)
        vv("m2", "b2", "PDF", A.mult)
        ts(T.OL[:, :], T.mq[:, :], float(NIL), None, [A.min], ["mq"], ["OL"])
        vv("m3", "al", k, A.mult)
        tt(T.RM[:, :], T.PD[:, 0:456].indirect(T.OL[:, 0:28]), T.MASK[:, :], A.mult, ["PD", "PDz", "OL", "MASK"], ["RM"])
        vv("k1", "KK", "m1", A.subtract)
        scan(T.SC[:, 1:225], T.RM[:, 0:448:2], T.RM[:, 1:448:2], 0.0, A.add, A.add, ["RM"], ["SC"])
        vv("k2", "m2", "m3", A.add)
        tt(T.dc[:, :], T.SC[:, 8:225:8], T.SC[:, 0:217:8], A.subtract, ["SC"], ["dc"])
        vv("k3", "k1", "k2", A.subtract)
        vcopy(T.RK1[:, :], T.lm[:, :], ["lm"], ["RK1"])
        n = "D%d" % (t + 1)
        vv(n, "dc", "k3", A.add)
        for e in (2, 0, 3, 1):
            ts(T["OF%d" % e][:, :], T[n][:, :], 4.0, float(e), [A.mult, A.add], [n], ["OF%d" % e])

    def send(t, h):
        a, b = HZ[h]
        dst = T.cores[(rank + 1 + t) % N]
        rid, pid, _ = topo.addr(dst)
        m = topo.mask(core, dst)
        waits("g", ["QZ%dh%d" % (t, h)], [])
        g.remote_dma(T["LZ%d" % t][:, a:b].bitcast(dt.uint8), T["QZ%d" % t][:, a:b].bitcast(dt.uint8),
                     T.sem["ar%d%dc" % (t, h)], T.sem.loc, pid, rid, m)
        g.remote_dma(T["LZS%d" % t][:, a:b], T["QZS%d" % t][:, a:b], T.sem["ar%d%ds" % (t, h)], T.sem.loc, pid, rid, m)
        cnt["loc"] = cnt.get("loc", 0) + 2 * len(topo.engines(core, dst))
        e = len(topo.engines(T.cores[(rank - 1 - t) % N], core))
        lastw["LZ%dh%d" % (t, h)] = ("ar%d%dc" % (t, h), e, None)
        lastw["LZS%dh%d" % (t, h)] = ("ar%d%ds" % (t, h), e, None)

    def mosaic(t):
        X = T["X%d" % t]

        def part(h, e):
            a, b = HZ[h]
            o, i = T.Z[:, 4 * a + e:4 * b:4], X[:, 0:1792].indirect(T["OF%d" % e][:, a // 16:b // 16])
            rd, wr = ["X%dh0" % t, "X%dh1" % t, "OF%d" % e], ["Zh%d.%d" % (h, e)]
            if e >= 2:
                act(o, i, F.Copy, rd, wr)
            else:
                vcopy(o, i, rd, wr)

        def pack(h):
            a, b = HZ[h]
            quant(T["QZ%d" % t][:, a:b], T["QZS%d" % t][:, a:b], T.Z[:, 4 * a:4 * b],
                  ["Zh%d.%d" % (h, e) for e in range(4)], ["QZ%dh%d" % (t, h)])
            send(t, h)

        for h in range(2):
            part(h, 2); part(h, 3)
        for h in range(2):
            part(h, 0); part(h, 1)
            pack(h)
        act(T["DR%d" % (t + 1)][:, :], T.IO4[:, :].indirect(T.OF0[:, 0:28]), F.Copy, ["IO4", "OF0"], ["DR%d" % (t + 1)])

    def join_list(t):
        sorted_row(t + 1)
        for h, s in enumerate("ab"):
            tt(T.RM[:, 224 * h:224 * h + 224], T.PD[:, 0:456].indirect(T.RK1[:, 14 * h:14 * h + 14]), T.MASK[:, 224 * h:224 * h + 224], A.mult,
               ["PD", "PDz", "RK1", "MASK", "RM"], ["RM" + s])
        for h, s in enumerate("ab"):
            o = 224 * h
            scan(T["SC" + s][:, 1:113], T.RM[:, o:o + 224:2], T.RM[:, o + 1:o + 224:2], 0.0, A.add, A.add, ["RM" + s], ["SC" + s])
        for h, s in enumerate("ab"):
            tt(T.ED[:, 14 * h:14 * h + 14], T["SC" + s][:, 8:113:8], T["SC" + s][:, 0:105:8], A.subtract, ["SC" + s], ["ED" + s])
        for h, s in enumerate("ab"):
            vcopy(T.EL[:, 14 * h:14 * h + 14], T.ED[:, 14 * h:14 * h + 14], ["ED" + s], ["EL" + s])

    def layer(t):
        for h in range(2):
            a, b = HZ[h]
            for w in range(4):
                mm(2 * w + h, b - a, T.WC[:, 128 * w:128 * w + 128], T.WS[:, 128 * w:128 * w + 128], T["LZ%d" % t][:, a:b], T["LZS%d" % t][:, a:b],
                   ["WC", "WS", "LZ%dh%d" % (t, h), "LZS%dh%d" % (t, h)])
        for w, h in ((0, 0), (1, 0), (0, 1), (2, 0), (1, 1), (3, 0), (2, 1), (3, 1)):
            a, b = HZ[h]
            bk = 2 * w + h
            act(T["HS%d" % w][:, a:b], T.PS[:, 512 * bk:512 * bk + b - a], F.Copy, ["bk%d" % bk], ["HS%dh%d" % (w, h)], scale=0.00390625)

    def join(t, h, ws=range(4)):
        a, b = H[h]
        for w in ws:
            tt(T["X%d" % (t + 1)][:, 4 * a + w:4 * b:4], T["HS%d" % w][:, 0:448].indirect(T.EL[:, a // 16:b // 16]),
               T["X%d" % t][:, 4 * a + w:4 * b:4], A.add, ["HS%dh0" % w, "HS%dh1" % w, "ELa", "ELb", "X%dh%d" % (t, h)], ["X%dh%d.%d" % (t + 1, h, w)])
        lastw["X%dh%d" % (t + 1, h)] = lastw["X%dh%d.%d" % (t + 1, h, ws[-1])]

    quant_x(0, 0)
    products(0)
    scores_head()
    quant_x(0, 1)
    products(1)
    vcopy(T.PW[:, :], T.PI[:, :], ["PI"], ["PW"])
    ts(T.OF0[:, :], T.PI[:, :], 4.0, None, [A.mult], ["PI"], ["OF0"])
    runmax(0); runmax(1)
    ts(T.MASK[:, :], T.MD[:, :], T.PM[:, 0:1], None, [A.is_equal], ["MD", "PM"], ["MASK"])
    vv("JP", "JW", "PW", A.add)
    ts(T.THR[:, :], T.IO4[:, 0:512:4], T.PF[:, 0:1], 0.5, [A.is_gt, A.subtract], ["IO4", "PF"], ["THR"])
    scores_tail()
    act(T.DR0[:, :], T.IO4[:, :].indirect(T.OF0[:, 0:28]), F.Copy, ["IO4", "OF0"], ["DR0"])

    for t in range(R):
        lists(t)
        pointers(t)
        mosaic(t)
        join_list(t)
        layer(t)
        if t == 0:
            quant(T.QV[:, :], T.QVS[:, :], T.VT[:, :], ["VT"], ["QV"])
        join(t, 0)
        if t < R - 1:
            join(t, 1, [0])
        quant_x(t + 1, 0)
        if t < R - 1:
            products(0)
            scores_head()
            join(t, 1, [1, 2])
            runmax(0)
            join(t, 1, [3])
            runmax(1)
            quant_x(t + 1, 1)
            products(1)
            scores_tail()
    dma("y", "sto0", T.op[:, :], T.DR3[0:128:16, :], ["DR3"], ["op"])
    dma("y", "sto1", T.oc[:, 0:1024], T.QX[:, 0:256].bitcast(dt.uint8), ["QXh0"], ["oc0"])
    mm(6, 256, T.QV[:, :], T.QVS[:, :], T.QX[:, 0:256], T.QXS[:, 0:256], ["QV", "QXh0"])
    act(T.YS[:, 0:256], T.PS[:, 3072:3328], F.Copy, ["bk6"], ["YS0"])
    dma("y", "sto2", T.y[:, 0:256], T.YS[:, 0:256], ["YS0"], ["y0"])
    join(R - 1, 1)
    quant_x(R, 1)
    mm(7, 192, T.QV[:, :], T.QVS[:, :], T.QX[:, 256:448], T.QXS[:, 256:448], ["QV", "QXh1"])
    dma("y", "sto3", T.oc[:, 1024:1792], T.QX[:, 256:448].bitcast(dt.uint8), ["QXh1"], ["oc1"])
    for k in range(4):
        dma("s" if k % 2 else "y", "sto%d" % (5 + k), T.osc[4 * k:4 * k + 4, :], T.QXS[32 * k:32 * k + 4, 0:448], ["QXh0", "QXh1"], ["osc%d" % k])
    vcopy(T.YS[:, 256:448], T.PS[:, 3584:3776], ["bk7"], ["YS1"])
    dma("s", "sto4", T.y[:, 256:448], T.YS[:, 256:448], ["YS1"], ["y1"])
    kn = known["g"]
    for s in sorted(cnt):
        if kn.get(s, 0) < cnt[s]:
            g.wait_ge(T.sem[s], cnt[s])
